import numpy as np, ml_dtypes
CORES = [23,119,17,113]
N = 4
BF = ml_dtypes.bfloat16
def gentries(a):
    return np.ascontiguousarray(a.reshape(8, 16, -1).transpose(0, 2, 1)).reshape(8, -1)
def gtable(e):
    e = np.asarray(e); return np.ascontiguousarray(e.reshape(8, -1, 16).transpose(0, 2, 1)).reshape(128, -1).astype(np.int32)
W, T, Z, VI, SH = 4096, 256, 4, 5, 5
STEP = (0, 1, 2, 3)
kk = np.arange(16)
def parts(rng):
    return rng.integers(0, 64, (N, 8, 16, W)), rng.integers(0, W, (N, 8, 4, T, 16)), rng.integers(450, 850, (N, 8, 16))
def pack(x, h, th):
    return {"x": np.ascontiguousarray(x.reshape(N, 128, W)).astype(np.float32).astype(BF), "hom": np.stack([gtable(a.reshape(8, -1)) for a in h]),
            "th": np.ascontiguousarray(th.reshape(N, 128, 1)).astype(np.int32)}
def lay(z, u, v):
    z, u, v = np.broadcast_arrays(z, u, v); s = np.arange(4)[:, None, None]
    return np.where((s == 0) | (s == z[..., None, :, :] + 1), u[..., None, :, :], v[..., None, :, :])
def setup_inputs(rng):
    return pack(*parts(rng))
def setup_inputs_spread(rng):
    x, h, th = parts(rng)
    x = (64 * np.exp2(-rng.integers(0, 7, (N, 8, 1, W))) * rng.random((N, 8, 16, W))).astype(np.int64)
    h = (W * rng.random((N, 8, 4, T, 16)) ** rng.integers(1, 5, (N, 8, 1, 1, 1))).astype(np.int64)
    th = (2017 * rng.random((N, 8, 16)) ** 3).astype(np.int64)
    return pack(x, np.minimum(h, W - 1), np.minimum(th, 2016))
def setup_inputs_ends(rng):
    x = 63 * rng.integers(0, 2, (N, 8, 16, W)); h = (W - 1) * rng.integers(0, 2, (N, 8, 4, T, 16)); th = 2016 * rng.integers(0, 2, (N, 8, 16))
    four = np.array([1, 2, W - 17, W - 2])
    for g in (0, 2, 4, 6, 7):
        e = 63 * rng.integers(0, 2, (N, 1)); x[:, g, :, 0] = e; x[:, g, :, W - 1] = 63 - e
        for j in range(4):
            x[:, g, :, int(four[j])] = np.where((j == 0) | (kk % 3 == j - 1), e, 63 - e)
    def zip3(j):
        return np.where(j < 3 * (Z // 3), j % 3, 3)
    a, b = kk < Z, kk >= 16 - Z
    top = np.where(a, zip3(kk), np.where(b, zip3(kk - 16 + Z), 1 + (kk & 1)))
    t2 = np.where(a, 0, np.where(b, 1, 2)); t3 = np.where(a, 2, np.where(b, 0, 1))
    late = np.where(b, 0, 2)
    turn = np.array([[0, 1, 2, 3], [0, 2, 1, 3], [0, 2, 3, 1]])
    def seq(z, j):
        return np.where((j == Z - 1) | (j % 3 == 0), z, np.where(j % 3 == 1, 0, 3 - z))
    def great(zl, zr, at):
        z = np.where(b, seq(zr, kk - 16 + Z), np.where(a, seq(zl, kk), zl))
        return np.where(a | b | (kk == at), four[turn[z]].T, lay(np.zeros((1, 16), np.int64), 0, W - 1)[:, 0])
    for g in (0, 7):
        for i, z in ((0, top), (1, late), (2, t3), (3, t2), (T - 5, t3), (T - 3, late), (T - 2, t2), (T - 1, top)):
            h[:, g, :, i] = lay(z[None, :], 0, W - 1)[:, 0]
        h[:, g, :, 4] = 0; h[:, g, :, T - 4] = W - 1
        for i, s in ((5, great(2, 1, 15 - Z)), (6, great(1, 2, Z)), (T - 7, great(1, 2, 15 - Z)), (T - 6, great(2, 1, Z))):
            h[:, g, :, i] = s
    th[:, ::2, 15] = 2016; th[:, 1::2, 15] = 0; th[:, ::2, 0] = 0; th[:, 1::2, 0] = 2016
    return pack(x, h, th)
def setup_inputs_corners(rng):
    x, h, th = parts(rng); own = 16 * np.arange(T)[:, None] + kk
    th = rng.choice(np.array([0, 1, 31, 600, 700, 2015, 2016]), (N, 8, 16))
    for q in range(N):
        for g in range(8):
            c = (q + g) % 8
            if c == 0: h[q, g] = 0
            if c == 1: h[q, g] = W - 1
            if c == 2: h[q, g] = own
            if c == 3: h[q, g, 0] = own; h[q, g, 1] = W - 1 - own; h[q, g, 2] = 0; h[q, g, 3] = W - 1
            if c == 4: h[q, g] = h[q, g, 0].copy()
            if c == 5: h[q, g] = rng.choice(np.array([Z, 16 * (T - 1) + 16 - Z, 0, W - 1]), (4, T, 16))
            if c == 6: h[q, g, :, ::2] = 0
            if c == 7: h[q, g, :, 1::2] = rng.choice(W - np.array([3, 5, 7, 9, 19, 21]), (4, T // 2, 16)); th[q, g] = rng.choice(np.array([0, 1, 31]), 16)
    return pack(x, h, th)
def setup_inputs_crowd(rng):
    x, h, th = parts(rng)
    x[:, :, 0] = (x[:, :, 0] & 62) | (np.arange(W) & 1); x[..., 2::4] = x[..., 0::4]; x[..., 3::4] = x[..., 1::4]
    p = rng.integers(0, 3, (N, 8, T)); q = (p + rng.integers(1, 3, (N, 8, T))) % 3
    n = np.array([T, T - 1, 0, 1, 31, 32, T // 2, T - 32])[(np.arange(8)[None, :] + np.arange(N)[:, None]) % 8]
    n[N - 1] = np.array([T, T - 1, T, T - 1, T - 1, T - 1, T - 1, T])
    q = np.where(np.argsort(rng.random((N, 8, T)), axis=-1) < n[..., None], q, p)
    at = rng.integers(Z, 17 - Z, (N, 8, T)); at[..., 0] = Z; at[..., T - 1] = 16 - Z
    u = 2 * rng.integers(0, W // 2, (N, 8, T, 16)); v = 2 * rng.integers(0, W // 2, (N, 8, T, 16)) + 1
    h = lay(np.where(kk < at[..., None], p[..., None], q[..., None]), u, v) ^ (2 * rng.integers(0, 2, (N, 8, 4, T, 16)))
    return pack(x, h, th)
def setup_inputs_ties(rng):
    x, h, th = parts(rng); top = rng.integers(1, 4, (N, 8, 1, 1)); top[:, 7] = 1; top[:, 0] = 3
    x = np.minimum((rng.random((N, 8, 16, W)) * (top + 1)).astype(np.int64), top)
    h[:, ::2, :, ::2] = lay(rng.integers(0, 4, (N, 4, T // 2, 16)), rng.integers(0, W, (N, 4, T // 2, 16)), rng.integers(0, W, (N, 4, T // 2, 16)))
    return pack(x, h, rng.integers(0, 21, (N, 8, 16)))
def check_inputs(d):
    bad = []
    for k, lo, hi in (("x", 0, 63), ("hom", 0, W - 1), ("th", 0, 2016)):
        a = np.asarray(d[k]).astype(np.float64)
        if not (np.min(a) >= lo and np.max(a) <= hi): bad.append("range of " + k)
        elif np.any(a != np.floor(a)): bad.append("whole numbers in " + k)
    return bad
def reference(x, hom, th):
    v = x.astype(np.float32).astype(np.int32).reshape(N, 8, 16, W)
    s = np.stack([gentries(a) for a in hom]).astype(np.int64).reshape(N, 8, 4, T, 16)
    t = th.astype(np.int64).reshape(N, 8, 1, 16); A = np.zeros((N, 8), np.int64)
    strand = np.arange(4)[None, None, :, None, None]
    for visit in range(VI):
        p = [np.take_along_axis(v, s[:, :, a].reshape(N, 8, 1, 16 * T), 3) for a in range(4)]
        def dist(a, b):
            return np.add.reduce(np.abs(p[a] - p[b]), axis=2).reshape(N, 8, T, 16).astype(np.int64)
        c = np.stack([dist(0, 1) + dist(2, 3), dist(0, 2) + dist(1, 3), dist(0, 3) + dist(1, 2)])
        L = np.argmin(np.add.reduce(c[..., :Z], axis=-1), axis=0); R = np.argmin(np.add.reduce(c[..., 16 - Z:], axis=-1), axis=0)
        cl = np.take_along_axis(c, L[None, ..., None], 0)[0]; cr = np.take_along_axis(c, R[None, ..., None], 0)[0]
        tot = np.stack([np.add.reduce(cl[..., :m], axis=-1) + np.add.reduce(cr[..., m:], axis=-1) for m in range(Z, 17 - Z)])
        meet = Z + np.argmin(tot, axis=0)
        right = kk >= meet[..., None]
        over = np.where(right, cr, cl) > t + (A & 31)[:, :, None, None]
        mate = strand ^ (np.where(right, R[..., None], L[..., None])[:, :, None] + 1)
        new = ((s * np.take_along_axis(s, mate, 2) >> SH) + s + 37 * kk) & (W - 1)
        s = np.where(over[:, :, None] & (mate < strand), new, s)
        sw = L != R
        s = np.where((sw[..., None] & right)[:, :, None], np.take_along_axis(s, mate, 2), s)
        at = (kk == meet[..., None]).reshape(N, 8, 1, 16 * T)
        v[..., :16 * T] = np.where(at, (v[..., :16 * T] + p[0]) >> 1, v[..., :16 * T])
        A = np.add.reduce(sw.astype(np.int64), axis=-1)
        s = np.stack([np.roll(s[:, :, a], STEP[a], axis=0) for a in range(4)], axis=2)
    return {"yx": v.reshape(N, 128, W).astype(np.float32).astype(BF), "ys": np.stack([gtable(a.reshape(8, -1)) for a in s]).astype(np.float32)}

@@ -1,0 +1,600 @@
+from concourse.bass import DstId, RemoteDMATransfer
+from concourse.mybir import AluOpType, ActivationFunctionType
+
+A = AluOpType
+F = ActivationFunctionType
+VI = 5
+STAR = False
+NJ = 2
+W = 128 // NJ
+FOLD = [] if STAR else [(a, b, c, 1024) for c in (0, 1024) for a, b in ((0, 2), (0, 1), (1, 2))]
+PAIRS = [(0, 1), (2, 3), (0, 2), (1, 3), (0, 3), (1, 2)]
+SLOT = {0: 0, 2: 1, 1: 2}
+VGATHER = [(0, 0, 2, 0)]
+CY, GCY, SCAT, PECY, FIX = 1.04, 1.56, 3.8, 0.52, 60
+FOLD_NS, BACK_NS, SEND_NS = 4000, 2500, 5000
+TRIES = [(a, b) for a in (40, 60, 100, 150) for b in (0, 4000, 8000)]
+
+SCRATCH = {}
+for _h in range(2):
+    SCRATCH["X%d" % _h] = ("sbuf", [128, 4096], "bfloat16")
+    SCRATCH["P%d" % _h] = ("sbuf", [128, 4 * 2048], "bfloat16")
+    SCRATCH["M%d" % _h] = ("sbuf", [128, 6 * 2048], "bfloat16")
+    for _v in range(VI):
+        SCRATCH["ST%d%d" % (_v, _h)] = ("sbuf", [128, 4, 128], "int32")
+    SCRATCH["RF%d" % _h] = ("sbuf", [128, 4, 128], "float32")
+    SCRATCH["LF%d" % _h] = ("sbuf", [128, 4, 128], "float32")
+    SCRATCH["U%d" % _h] = ("sbuf", [128, 4, 128], "uint16")
+    SCRATCH["thi%d" % _h] = ("sbuf", [128, 4], "int32")
+    SCRATCH["thr%d" % _h] = ("sbuf", [128, 4], "float32")
+for _n, _w, _d in [
+    ("bx", 128, "bfloat16"), ("sg", 128, "bfloat16"), ("cb", 128, "bfloat16"), ("at", 128, "bfloat16"),
+    ("acc", 4, "float32"), ("ai", 4, "int32"), ("ixp", 8, "uint16"), ("ixx", 8, "uint16"),
+    ("pb", 128, "bfloat16"), ("bs", 128, "bfloat16"), ("br", 128, "bfloat16"),
+    ("CI", 8, "int32"), ("CF", 8, "float32"), ("CX", 16, "float32"), ("J", 144, "float32"), ("JB", 128, "float32"),
+    ("JG", 128, "float32"), ("Wd", 144, "bfloat16"), ("NWd", 144, "bfloat16"), ("MI", 144, "bfloat16"),
+    ("ID", 640, "bfloat16"), ("bm", 8, "float32"), ("BC", 1024, "bfloat16"), ("AW", 128, "float32"),
+    ("eq", 8, "float32"), ("lam", 12, "float32"), ("WT", 512, "bfloat16"), ("RX", 384, "bfloat16"),
+    ("C256", 8, "bfloat16"), ("NEG", 128, "bfloat16"),
+]:
+    SCRATCH[_n] = ("sbuf", [128, _w], _d)
+for _n, _w, _d in [("MS", 3, "float32"), ("LM", 3, "float16"), ("FM", 3, "float16"), ("ps", 3, "bfloat16"), ("sq", 3, "bfloat16"),
+                   ("DD", 2, "float32"), ("PR", 2, "int32"), ("WZ", 3, "float32"), ("WB", 11, "bfloat16")]:
+    SCRATCH[_n] = ("sbuf", [128, _w, 128], _d)
+SCRATCH["SR"] = ("sbuf", [128, 3, 3], "float32")
+SCRATCH["AE"] = ("sbuf", [128, 3, 3, 12], "float32")
+SCRATCH["LH"] = ("sbuf", [128, 2, 3, 12], "float32")
+SCRATCH["LQ"] = ("sbuf", [128, 4, 3, 12], "float32")
+SCRATCH["AR"] = ("sbuf", [128, 11, 16], "float32")
+SCRATCH["pC"] = ("psum", [128, 2048 if STAR else 1536], "float32")
+for _n in ("pM", "pD", "pK", "pV") + (() if STAR else ("pO",)):
+    SCRATCH[_n] = ("psum", [128, 4, 128], "float32")
+
+SEMAPHORES = ["cV", "cS", "cP", "cG", "thl", "sent", "out", "hsent"]
+for _h in range(2):
+    SEMAPHORES += ["xl%d" % _h, "hl%d" % _h, "tw%d" % _h, "lf%d" % _h]
+    SEMAPHORES += ["ar%d%d%d%d" % (_v, _h, _j, _s) for _v in range(VI) for _j in range(NJ) for _s in range(4)]
+    SEMAPHORES += ["ha%d%d" % (_f, _h) for _f in range(len(FOLD))] + ["hb%d%d" % (_f, _h) for _f in range(len(FOLD))]
+
+
+def helpers_of(core, T, topo):
+    return [c for c in topo.cores_of(core) if T.rank_of(c) is None and topo.die(c) == topo.die(core)]
+
+
+def bits(engines):
+    m = 0
+    for e in engines:
+        m |= 1 << e
+    return m
+
+
+def helper_slot(T, v, h, f):
+    n = (2 * v + h) * ((len(FOLD) + 2) // 3) + f // 3
+    name, j = [("P0", n), ("P1", n - 4), ("M0", n - 8), ("M1", n - 14)][0 if n < 4 else 1 if n < 8 else 2 if n < 14 else 3]
+    return T[name][:, j * 2048:j * 2048 + FOLD[f][3]]
+
+
+def build(g, core, T, topo):
+    ops, lastw, readers, cur = [], {}, {}, [-2, 0]
+    rank = T.rank_of(core)
+    sem = T.sem
+
+    def op(eng, dur, fn, r=(), w=(), banks=(), lat=0, sig=None, tag=None):
+        o = {"eng": eng, "dur": dur, "fn": fn, "banks": banks, "lat": lat, "sig": sig, "deps": set(), "i": len(ops), "tag": tag,
+             "u": cur[0], "c": cur[1], "h": cur[0] % 2}
+        cur[1] += 1
+        for k in r:
+            if k in lastw:
+                o["deps"].update(lastw[k])
+        for k in w:
+            o["deps"].update(lastw.get(k, ()))
+            o["deps"].update(readers.get(k, ()))
+        for k in r:
+            readers.setdefault(k, []).append(o["i"])
+        for k in w:
+            lastw[k] = [o["i"]]
+            readers[k] = []
+        o["deps"].discard(o["i"])
+        ops.append(o)
+        return o
+
+    def vec(n, fn, r, w, banks=()):
+        return op("V", FIX + max(64, n) * CY, lambda e: fn(g.vector), r, w, banks)
+
+    def ts(out, in0, s1, s2, o0, o1, n, r, w, banks=()):
+        if o1 is None:
+            return vec(n, lambda q: q.tensor_scalar(out, in0, s1, None, o0), r, w, banks)
+        return vec(n, lambda q: q.tensor_scalar(out, in0, s1, s2, o0, o1), r, w, banks)
+
+    def tt(out, in0, in1, o, n, r, w, banks=()):
+        return vec(n, lambda q: q.tensor_tensor(out, in0, in1, o), r, w, banks)
+
+    def cp(out, in_, n, r, w, banks=()):
+        return vec(n, lambda q: q.tensor_copy(out, in_), r, w, banks)
+
+    def act(out, in_, func, n, r, w, banks=(), **kw):
+        return op("S", FIX + 20 + max(64, n) * CY, lambda e: g.scalar.activation(out, in_, func, **kw), r, w, banks)
+
+    def pe(mms, r, w, banks):
+        def fn(e):
+            last = None
+            for m in mms:
+                last = g.tensor.matmul(m[0], m[1], m[2], m[3], m[4])
+            return last
+        return op("P", sum([max(64, m[5]) * PECY + 5 for m in mms]), fn, r, w, banks, lat=60)
+
+    def group(out, terms, n):
+        return [(out, a, b, i == 0, i == len(terms) - 1, n) for i, (a, b) in enumerate(terms)]
+
+    def dma(eng, out, in_, s, total, r, w, lat):
+        q = g.sync if eng == "Y" else g.scalar
+        return op(eng, 120, lambda e: q.dma_start(out, in_).then_inc(sem[s], 16), r, w, lat=lat, sig=(s, total))
+
+    def iota(out, pattern, base, cm, w, n, flag=True):
+        if flag:
+            return op("G", 160 + 2 * n * CY, lambda e: g.iota(out, pattern, base, cm, allow_small_or_imprecise_dtypes=True), (), w)
+        return op("G", 160 + 2 * n * CY, lambda e: g.iota(out, pattern, base, cm), (), w)
+
+    for h in range(2):
+        for s in range(4):
+            for t in range(2):
+                dma("Y" if (h or t) else "S", T["ST0%d" % h][64 * t:64 * t + 64, s, :],
+                    T.hom[64 * h:64 * h + 64, 256 * s + 128 * t:256 * s + 128 * t + 128], "hl%d" % h, 128, (), [("STl", h, s, t)], 2200)
+            if s == 0:
+                for t in range(2):
+                    dma("Y" if (h or t) else "S", T["X%d" % h][64 * t:64 * t + 64, :], T.x[64 * h:64 * h + 64, :], "xl%d" % h, 32, (),
+                        [("Xl", h, t)], 4000)
+    CI, CF, CX, J, ID, AR, WB, BC = T.CI, T.CF, T.CX, T.J, T.ID, T.AR, T.WB, T.BC
+    iota(CI[:, 0:1], [[0, 1]], 0, 1, ["CI0"], 1, False)
+    iota(J[:], [[1, 144]], 0, 0, ["J"], 144)
+    iota(T.JB[:], [[16, 8], [0, 16]], 0, 0, ["JB"], 128)
+    iota(T.AE[:, 0], [[0, 4], [1, 9]], 4, 0, ["AE0"], 36)
+    iota(T.AE[:, 1], [[1, 4], [1, 9]], 5, 0, ["AE1"], 36)
+    iota(T.C256[:], [[256, 8]], 0, 0, ["C256"], 8)
+    iota(T.JG[:], [[0, 2], [1, 4], [0, 16]], 0, 0, ["JG"], 128)
+    for h in range(2):
+        for t in range(2):
+            op("G", 600, lambda e, h=h, t=t: g.dma_start(T["thi%d" % h][64 * t:64 * t + 64, 0:1], T.th[64 * h:64 * h + 64, :],
+                                                          allow_slow_non_contiguous=True).then_inc(sem.thl, 16),
+               (), [("thl", h, t)], lat=3000, sig=("thl", 64))
+    q0 = CI[:, 0:1]
+    ts(CI[:, 1:2], q0, 15, None, A.bitwise_and, None, 1, ["CI0"], ["CI1"])
+    ts(CI[:, 2:3], q0, 2, 3, A.arith_shift_right, A.bitwise_and, 1, ["CI0"], ["CI2"])
+    ts(CI[:, 3:4], q0, 3, None, A.bitwise_and, None, 1, ["CI0"], ["CI3"])
+    ts(CI[:, 4:5], q0, 112, None, A.bitwise_and, None, 1, ["CI0"], ["CI4"])
+    ts(CI[:, 5:6], q0, 4, 3, A.arith_shift_right, A.bitwise_and, 1, ["CI0"], ["CI5"])
+    ts(CI[:, 6:7], q0, 64, None, A.bitwise_and, None, 1, ["CI0"], ["CI6"])
+    cp(CF[:, 0:7], CI[:, 0:7], 7, ["CI%d" % i for i in range(7)], ["CF"])
+    qf, kf, Lf, Rf, bf, gf, tf = [CF[:, i:i + 1] for i in range(7)]
+    ts(T.Wd[:], J[:], 15.0, bf, A.subtract, A.is_equal, 144, ["J", "CF"], ["Wd"])
+    for i, c in enumerate((1.0, 2.0, 0.5, -0.5, -1.0)):
+        ts(ID[:, 128 * i:128 * i + 128], J[:, 0:128], qf, c, A.is_equal, A.mult, 128, ["J", "CF"], ["ID%d" % i])
+    I1, I2, IH, NIH, NI = [ID[:, 128 * i:128 * i + 128] for i in range(5)]
+    ts(T.NWd[:], T.Wd[:], -1.0, None, A.mult, None, 72, ["Wd"], ["NWd"])
+    ts(T.MI[:], T.Wd[:], kf, None, A.mult, None, 72, ["Wd", "CF"], ["MI"])
+    ts(T.bm[:], T.JB[:, 0:128:16], bf, None, A.is_equal, None, 8, ["JB", "CF"], ["bm"])
+    eq, lam = T.eq, T.lam
+    ts(eq[:, 0:3], J[:, 0:3], Lf, None, A.is_equal, None, 3, ["J", "CF"], ["eqL"])
+    ts(eq[:, 4:7], J[:, 0:3], Rf, None, A.is_equal, None, 3, ["J", "CF"], ["eqR"])
+    tt(lam[:, 0:3], eq[:, 0:3], eq[:, 4:7], A.subtract, 3, ["eqL", "eqR"], ["lam"])
+    tt(lam[:, 8:11], lam[:, 0:3], lam[:, 0:3], A.mult, 3, ["lam"], ["lam2"])
+    ts(lam[:, 8:11], lam[:, 8:11], 0.5, None, A.mult, None, 3, ["lam2"], ["lam2"])
+    tt(lam[:, 4:7], lam[:, 8:11], eq[:, 0:3], A.add, 3, ["lam2", "eqL"], ["Fc"])
+    ts(lam[:, 5:6], lam[:, 4:5], lam[:, 6:7], -1.0, A.add, A.mult, 1, ["Fc"], ["Fc1"])
+    ts(lam[:, 5:6], lam[:, 5:6], 1.0, None, A.add, None, 1, ["Fc1"], ["Fc1"])
+    tt(lam[:, 3:4], Lf, Rf, A.not_equal, 1, ["CF"], ["sw"])
+    ts(lam[:, 7:8], lam[:, 3:4], -0.5, None, A.mult, None, 1, ["sw"], ["Wc"])
+    for i in range(8):
+        ts(BC[:, 128 * i:128 * i + 128], T.JB[:], bf, lam[:, i:i + 1], A.is_equal, A.mult, 128,
+           ["JB", "CF", "lam", "sw", "Fc", "Fc1", "Wc"], ["BC%d" % i])
+    bc = [BC[:, 128 * i:128 * i + 128] for i in range(8)]
+    bck = ["BC%d" % i for i in range(8)]
+    ts(T.AW[:], T.JG[:], gf, lam[:, 3:4], A.is_equal, A.mult, 128, ["JG", "CF", "sw"], ["AW"])
+    ts(CX[:, 0:1], kf, 4.0, None, A.is_lt, None, 1, ["CF"], ["CX0"])
+    ts(CX[:, 1:2], kf, 12.0, None, A.is_ge, None, 1, ["CF"], ["CX1"])
+    ts(CX[:, 2:3], kf, 16.0, None, A.mult, None, 1, ["CF"], ["CX2"])
+    ts(CX[:, 3:4], tf, 32.0, CX[:, 2:3], A.mult, A.add, 1, ["CF", "CX2"], ["CX3"])
+    ts(CX[:, 4:5], kf, 37.0, None, A.mult, None, 1, ["CF"], ["CX4"])
+    vec(88, lambda q: q.memset(AR[:], 0.0), (), ["AR"])
+    vec(64, lambda q: q.memset(T.NEG[:], -128.0), (), ["NEG"])
+    SR = T.SR
+    vec(9, lambda q: q.memset(SR[:], 0.0), (), ["SR"])
+    for i, (a, c) in enumerate(((SR[:, 0, 0:2], -1.0), (SR[:, 1, 2:3], -1.0), (SR[:, 1, 0:1], 1.0), (SR[:, 2, 1:3], 1.0))):
+        vec(2, lambda q, a=a, c=c: q.memset(a, c), ["SR"], ["SR%d" % i])
+    srk = ["SR0", "SR1", "SR2", "SR3", "AR"]
+    ts(AR[:, 0:3, 0:3], SR[:], CX[:, 0:1], None, A.mult, None, 9, srk + ["CX0"], ["AR0"])
+    ts(AR[:, 0:3, 3:6], SR[:], CX[:, 1:2], None, A.mult, None, 9, srk + ["CX1"], ["AR1"])
+    AE, LH, LQ = T.AE, T.LH, T.LQ
+    ts(AE[:, 2], AE[:, 1], 13.0, -9.0, A.is_ge, A.mult, 36, ["AE1"], ["AE2"])
+    tt(AE[:, 2], AE[:, 2], AE[:, 1], A.add, 72, ["AE1", "AE2"], ["AE2"])
+    tt(LH[:, 0], AE[:, 0], AE[:, 2], A.min, 72, ["AE0", "AE2"], ["LH0"])
+    tt(LH[:, 1], AE[:, 0], AE[:, 2], A.max, 72, ["AE0", "AE2"], ["LH1"])
+    for i in range(2):
+        ts(LQ[:, i], LH[:, i], kf, None, A.is_le, None, 36, ["LH%d" % i, "CF"], ["LQ%d" % i])
+        ts(LQ[:, 2 + i], LH[:, i], kf, None, A.is_equal, None, 36, ["LH%d" % i, "CF"], ["LQ%d" % (2 + i)])
+    tt(AR[:, 3:6, 0:12], LQ[:, 0], LQ[:, 1], A.subtract, 72, ["LQ0", "LQ1", "AR"], ["AR2"])
+    tt(AR[:, 6:9, 0:12], LQ[:, 2], LQ[:, 3], A.subtract, 72, ["LQ2", "LQ3", "AR"], ["AR3"])
+    for i in range(2):
+        c = 4 * i
+        ts(AR[:, 9, 3 * i:3 * i + 2], eq[:, c + 1:c + 3], eq[:, c:c + 1], -1.0, A.subtract, A.mult, 2, ["eqL", "eqR", "AR"], ["AR4%d" % i])
+        tt(AR[:, 9, 3 * i + 2:3 * i + 3], eq[:, c + 1:c + 2], eq[:, c + 2:c + 3], A.subtract, 2, ["eqL", "eqR", "AR"], ["AR5%d" % i])
+    ts(AR[:, 10, :], J[:, 0:16], kf, None, A.is_ge, None, 16, ["J", "CF", "AR"], ["AR6"])
+    ark = ["AR0", "AR1", "AR2", "AR3", "AR40", "AR41", "AR50", "AR51", "AR6", "bm"]
+    for b in range(8):
+        ts(WB[:, :, 16 * b:16 * b + 16], AR[:], T.bm[:, b:b + 1], None, A.mult, None, 176, ark, ["WB%d" % b])
+    wbk = ["WB%d" % b for b in range(8)]
+    pD, pM, pK, pV, pC = T.pD, T.pM, T.pK, T.pV, T.pC
+    cp(T.WZ[:], WB[:, 0:3, :], 384, wbk, ["WZ"])
+    alld = [("D", i, j) for i in range(4) for j in range(NJ)]
+    pe([(pD[:, j, :], WB[:, 6 + j, :], I1, True, True, 128) for j in range(4)], wbk + ["ID0"], alld, ["D"])
+    act(T.WT[:], pD[:], F.Copy, 512, alld, ["WT"], ["D"])
+    RT = WB[:, 10, :]
+    for i, c in enumerate((0.5, -1.0, -0.5)):
+        ts(T.RX[:, 128 * i:128 * i + 128], RT, c, None, A.mult, None, 64, wbk, ["RX%d" % i])
+    RTH, NRT, NRTH = [T.RX[:, 128 * i:128 * i + 128] for i in range(3)]
+    for h in range(2):
+        cp(T["thr%d" % h][:, 0:1], T["thi%d" % h][:, 0:1], 1, [("thl", a, b) for a in range(2) for b in range(2)], [("thr", h)])
+
+    others = [T.cores[(rank + s) % len(T.cores)] for s in range(4)]
+    helpers = helpers_of(core, T, topo)
+    far = [s for s in (1, 2, 3) if topo.chip(others[s]) != topo.chip(core)]
+    masks, used = {}, []
+    for i, s in enumerate(far):
+        e = topo.engines(core, others[s])
+        e = e[i * len(e) // len(far):(i + 1) * len(e) // len(far)]
+        masks[s] = e
+        used += e
+    near = [s for s in (1, 2, 3) if s not in far]
+    for i, s in enumerate(near):
+        e = [x for x in topo.engines(core, others[s]) if x not in used]
+        masks[s] = e[i * len(e) // len(near):(i + 1) * len(e) // len(near)]
+    sent = sum([len(masks[s]) for s in (1, 2, 3)])
+    crot = [0]
+
+    def pairs_of_piece(v, h, j, xr):
+        X, P, M, U = T["X%d" % h], T["P%d" % h], T["M%d" % h], T["U%d" % h]
+        jc, lo = j * NJ // 2, 1024 * j
+        for s in (0, 2, 1, 3):
+            out = P[:, 2048 * s + lo:2048 * s + lo + 1024]
+            win = X[:, 0:4096].indirect(U[:, s, 64 * j:64 * j + 64])
+            rk = xr + [("U", h, jc, s)]
+            if STAR and s:
+                tt(out, win, P[:, lo:lo + 1024], A.subtract, 1024 * GCY, rk + [("P", h, 0, j)], [("P", h, s, j)])
+                pi = PAIRS.index((0, s))
+                act(M[:, 2048 * pi + lo:2048 * pi + lo + 1024], out, F.Abs, 1024, [("P", h, s, j)], [("M", h, pi, j)])
+            elif (v, h, s, j) in VGATHER:
+                cp(out, win, 1024 * GCY, rk, [("P", h, s, j)])
+            else:
+                act(out, win, F.Copy, 1024 * GCY, rk, [("P", h, s, j)])
+        for f, (a, b, c0, n) in enumerate(FOLD):
+            if (c0 + n - 1) // 1024 != j:
+                continue
+            hc = helpers[f % len(helpers)]
+            rid, pid, _ = topo.addr(hc)
+            pi = PAIRS.index((a, b))
+            js = range(c0 // 1024, (c0 + n) // 1024)
+            pk = [("P", h, s, i) for s in (a, b) for i in js]
+            mk = [("M", h, pi, i) for i in js]
+            tr = RemoteDMATransfer(dst_ids=[DstId(rid=rid, pnc=pid)], dma_engine_mask=topo.mask(core, hc), remote_sem=sem["ha%d%d" % (f, h)],
+                                   srcs=[P[:, 2048 * a + c0:2048 * a + c0 + n], P[:, 2048 * b + c0:2048 * b + c0 + n]],
+                                   dsts=[helper_slot(T, v, h, f)], alu_op=2)
+            op("G", 1000, lambda e, tr=tr: g.remote_dma_fused([tr], local_sem=sem["lf%d" % h]), pk, mk + [("f1", v, h, f)],
+               sig=(None, 0), tag=(v, h, f))
+            op("D", FOLD_NS * n / 2048, None, pk + [("f1", v, h, f)], [("f2", v, h, f)],
+               sig=("lf%d" % h, (v + 1) * len(topo.engines(core, hc)) * len(FOLD)))
+            op("E", 0, None, [("f2", v, h, f)], mk, lat=BACK_NS + FOLD_NS * n / 4096,
+               sig=("hb%d%d" % (f, h), (v + 1) * len(topo.engines(hc, core))))
+        if STAR:
+            for a, b in ((1, 2), (2, 3), (1, 3)):
+                pi = PAIRS.index((a, b))
+                base = 1024 * (crot[0] % 2)
+                bk = ["C%d" % (base // 512), "C%d" % (base // 512 + 1)]
+                crot[0] += 1
+                mm = []
+                for i in (0, 512):
+                    mm += group(pC[:, base + i:base + i + 512], [(I1, P[:, 2048 * a + lo + i:2048 * a + lo + i + 512]),
+                                                                 (NI, P[:, 2048 * b + lo + i:2048 * b + lo + i + 512])], 512)
+                pe(mm, [("P", h, a, j), ("P", h, b, j), "ID0", "ID4"], bk, bk)
+                act(M[:, 2048 * pi + lo:2048 * pi + lo + 1024], pC[:, base:base + 1024], F.Abs, 1024, bk, [("M", h, pi, j)], bk)
+        for b in range(1, 4):
+            mine = [a for a in range(b) if not [x for x in FOLD if x[0:2] == (a, b) and x[2] <= lo < x[2] + x[3]]]
+            if not mine or STAR:
+                continue
+            crot[0] += 1
+            for c0, n, base, bk in ([(lo, 1024, 0, ["C0", "C1"])] if crot[0] % 2 else [(lo, 512, 1024, ["C2"]), (lo + 512, 512, 0, ["C0"])]):
+                pe([(pC[:, base + i:base + i + 512], I1, P[:, 2048 * b + c0 + i:2048 * b + c0 + i + 512], True, True, 512)
+                    for i in range(0, n, 512)], [("P", h, b, j), "ID0"], bk, bk)
+                for a in mine:
+                    pi = PAIRS.index((a, b))
+                    tt(M[:, 2048 * pi + c0:2048 * pi + c0 + n], pC[:, base:base + n], P[:, 2048 * a + c0:2048 * a + c0 + n],
+                       A.max, n, bk + [("P", h, a, j)], [("M", h, pi, j)], bk)
+        for p in range(3):
+            terms = [(T.Wd[:, 15 - k:143 - k], M[:, 2048 * pi + lo + k:2048 * pi + lo + 1024:16])
+                     for pi in (2 * p, 2 * p + 1) for k in range(16)]
+            pe(group(pM[:, SLOT[p], 64 * j:64 * j + 64], terms, 64), [("M", h, 2 * p, j), ("M", h, 2 * p + 1, j), "Wd"], [("pM", p, j)], ["M"])
+
+    def chunk(v, h, j, xr):
+        X, P, U, ST = T["X%d" % h], T["P%d" % h], T["U%d" % h], T["ST%d%d" % (v, h)]
+        last = v == VI - 1
+        c = slice(W * j, W * j + W)
+        ci = slice(W // 16 * j, W // 16 * (j + 1))
+        pieces = range(2 * j // NJ, 2 * (j + 1) // NJ)
+        thr = T["thr%d" % h][:, 0:1]
+        sk = [("ST", v, h, j, s) for s in range(4)]
+        dk = [("D", i, j) for i in range(4)]
+        pO, OB = (pM[:, 3, c], "M") if STAR else (T.pO[:, 0, c], "O")
+
+        def k(name):
+            return (name, j)
+        for i, s in enumerate(() if STAR else (0, 2, 1, 3)):
+            pe([(pO, T.NWd[:, 15 - r:143 - r], P[:, 2048 * s + 16 * W * j + r:2048 * s + 16 * W * (j + 1):16], i == 0 and r == 0, False, W)
+                for r in range(16)], [("P", h, s, q) for q in pieces] + ["NWd"], ["O"], [OB])
+        MS, cb, at = T.MS[:, :, c], T.cb[:, c], T.at[:, c]
+        act(MS, pM[:, 0:3, c], F.Copy, 3 * W, [("pM", p, q) for p in range(3) for q in pieces], [k("MS")], ["M"])
+        d = [pD[:, i, c] for i in range(4)]
+        d3 = pD[:, 0:3, c]
+        pe(group(d[0], [(T.WZ[:, p, :], T.MS[:, SLOT[p], c]) for p in range(3)], 4 * W), ["WZ", k("MS")], dk[0:1], ["D"])
+        act(T.sg[:, c], d[0], F.Sign, W, dk[0:1], [k("sg")], ["D"], bias=0.5)
+        pe(group(d[3], [(T.WT[:, 384:512], T.sg[:, c])], W), ["WT", k("sg")], dk[3:], ["D"])
+        act(cb, d[3], F.Relu, W + 130, dk[3:], [k("cb"), k("acc")], ["D"], bias=-3.0, accum_out=T.acc[:, j:j + 1])
+        pe([(d[SLOT[p]], bc[p], cb, True, True, W) for p in range(3)], bck + [k("cb")], dk[0:3], ["D"])
+        tt(T.LM[:, :, c], d3, MS, A.mult, 3 * W, dk[0:3] + [k("MS")], [k("LM")], ["D"])
+        mm = []
+        for q in range(3):
+            mm += group(d[q], [(WB[:, 3 + q, :], T.LM[:, i, c]) for i in range(3)], W)
+        pe(mm, wbk + [k("LM")], dk[0:3], ["D"])
+        act(T.ps[:, :, c], d3, F.Sign, 3 * W, dk[0:3], [k("ps")], ["D"], bias=0.5)
+        pe(group(d[3], [(T.WT[:, 128 * q:128 * q + 128], T.ps[:, q, c]) for q in range(3)], W), ["WT", k("ps")], dk[3:], ["D"])
+        act(at, d[3], F.Relu, W, dk[3:], [k("at")], ["D"], bias=-7.0)
+        ix = pD[:, 3, W * j:W * j + W // 16]
+        pe(group(ix, [(T.MI[:, 15 - r:143 - r], T.at[:, W * j + r:W * j + W:16]) for r in range(16)] + [(I1, T.C256[:, ci])], 64),
+           ["MI", k("at"), "ID0", "C256"], dk[3:], ["D"])
+        ts(T.ixp[:, ci], ix, CX[:, 2:3], None, A.add, None, 8, dk[3:] + ["CX2"], [k("ixp")], ["D"])
+        ts(T.ixx[:, ci], ix, CX[:, 3:4], None, A.add, None, 8, dk[3:] + ["CX3"], [k("ixx")], ["D"])
+        if j == NJ - 1:
+            js = range(NJ)
+            act(T.pb[:], P[:, 0:2048].indirect(T.ixp[:]), F.Copy, 128 * GCY, [("P", h, 0, 0), ("P", h, 0, 1)] + [("ixp", q) for q in js], ["pb"])
+            xk, ik = [("X", h, 0), ("X", h, 1)], [("ixx", q) for q in js]
+            tt(T.bs[:], X[:, 0:4096].indirect(T.ixx[:]), T.pb[:], A.add, 128 * GCY, xr + ik + ["pb"], ["bs"])
+            act(T.br[:], T.bs[:], F.Identity, 128, ["bs"], ["br"], scale=0.5, bias=127.8)
+            tt(X[:, 0:4096].indirect(T.ixx[:]), T.br[:], T.NEG[:], A.add, 128 * SCAT, ["br", "NEG"] + ik, xk + (xr if v == 0 else []))
+            for t in range(2):
+                mine = X[64 * t:64 * t + 64, 2048 * t:2048 * t + 2048]
+                if last:
+                    dma("Y", T.yx[64 * h:64 * h + 64, 2048 * t:2048 * t + 2048], mine, "out", 16 * (4 + 16 * NJ), [("X", h, t)], (), 3500)
+                else:
+                    dma("Y", X[64 - 64 * t:128 - 64 * t, 2048 * t:2048 * t + 2048], mine, "tw%d" % h, 32 * (v + 1), (), [("X", h, t)], 3500)
+        mm = []
+        for i, q in enumerate((0, 2, 3)):
+            mm += group(d[i], [(bc[q], cb), (RT, at)], W)
+        pe(mm, bck + wbk + [k("cb"), k("at")], dk[0:3], ["D"])
+        act(T.sq[:, :, c], d3, F.Square, 3 * W, dk[0:3], [k("sq")], ["D"])
+        sq = [T.sq[:, i, c] for i in range(3)]
+        mm = group(pK[:, 0, c], [(bc[4], cb), (RTH, at), (NIH, sq[0])], W)
+        mm += group(pK[:, 1, c], [(bc[6], cb), (RTH, at), (NIH, sq[1])], W)
+        mm += group(pK[:, 2, c], [(bc[5], cb), (NRT, at), (IH, sq[0]), (IH, sq[1])], W)
+        mm += group(pK[:, 3, c], [(bc[7], cb), (NRTH, at), (IH, sq[2])], W)
+        K = k("K")
+        pe(mm, bck + [k("cb"), k("at"), k("sq"), "RX0", "RX1", "RX2", "ID2", "ID3"], [K], ["K"])
+        tt(T.FM[:, :, c], pK[:, 0:3, c], MS, A.mult, 3 * W, [K, k("MS")], [k("FM")], ["K"])
+        pe([(pO, I1 if STAR else I2, T.FM[:, i, c], STAR and i == 0, i == 2, W) for i in range(3)], [k("FM"), "ID0", "ID1"], ["O"], [OB])
+        ov = pV[:, 2, c]
+        ts(ov, pO, thr, None, A.is_gt, None, W, ["O", ("thr", h)], [k("ov")], [OB, "V"])
+        if not last and j == NJ - 1:
+            a = pD[:, 3, W * j + 16:W * j + 17]
+            pe(group(a, [(T.AW[:], T.acc[:, q:q + 1]) for q in range(NJ)], 256), ["AW"] + [("acc", q) for q in range(NJ)], dk[3:], ["D"])
+            cp(T.ai[:, 0:1], a, 1, dk[3:], ["ai"], ["D"])
+            ts(T.ai[:, 0:1], T.ai[:, 0:1], 31, None, A.bitwise_and, None, 1, ["ai"], ["ai"])
+            tt(thr, T.ai[:, 0:1], T["thi%d" % h][:, 0:1], A.add, 1, ["ai"], [("thr", h)])
+        DD, PR, ab, f02 = T.DD[:, :, c], T.PR[:, :, c], pV[:, 0:2, c], pK[:, 0:2, c]
+        lo, mid, hi = ST[:, 0:2, c], ST[:, 1:3, c], ST[:, 2:4, c]
+        kd, kp, ka, kh = k("DD"), k("PR"), k("ab"), [k("h0"), k("h1")]
+        tt(DD, hi, mid, A.subtract, 4 * W, sk[1:], [kd])
+        tt(ab, f02, DD, A.mult, 2 * W, [K, kd], [ka], ["K", "V"])
+        tt(hi, hi, ab, A.subtract, 2 * W, [ka], sk[2:], ["V"])
+        tt(mid, mid, ab, A.add, 2 * W, [ka], sk[1:3], ["V"])
+        tt(PR, lo, hi, A.mult, 4 * W, sk, [kp])
+        ts(PR, PR, 5, None, A.arith_shift_right, None, 2 * W, (), [kp])
+        ts(PR, PR, CX[:, 4:5], None, A.add, None, 2 * W, ["CX4"], [kp])
+        for i in range(2):
+            tt(pV[:, i, c], ov, T.PR[:, i, c], A.mult, W, [k("ov"), kp, ka], [kh[i]], ["V"])
+        tt(hi, hi, ab, A.add, 2 * W, kh, sk[2:] + [ka], ["V"])
+        ts(hi, hi, 4095, None, A.bitwise_and, None, 2 * W, (), sk[2:])
+        tt(DD, hi, lo, A.subtract, 4 * W, sk, [kd])
+        for i in range(2):
+            tt(pV[:, i, c], pK[:, 3, c], T.DD[:, i, c], A.mult, W, [K, kd, ka], [kh[i]], ["K", "V"])
+        R = T["RF%d" % h] if last else ST
+        tt(R[:, 0:2, c], lo, ab, A.add, 2 * W, kh, sk[0:2], ["V"])
+        if not last:
+            cp(U[:, 0, c], R[:, 0, c], W, [sk[0]], [("U", h, j, 0)])
+        mid, rhi = R[:, 1:3, c], R[:, 2:4, c]
+        tt(rhi, hi, ab, A.subtract, 2 * W, kh, sk[2:], ["V"])
+        tt(DD, rhi, mid, A.subtract, 4 * W, sk[1:], [kd])
+        tt(ab, f02, DD, A.mult, 2 * W, [K, kd], [ka] + kh, ["K", "V"])
+        tt(mid, mid, ab, A.add, 2 * W, [ka], sk[1:3], ["V"])
+        tt(rhi, rhi, ab, A.subtract, 2 * W, [ka], sk[2:], ["V"])
+        NX = T["LF%d" % h] if last else T["ST%d%d" % (v + 1, h)]
+        ar = ["ar%d%d%d%d" % (v, h, j, s) for s in range(4)]
+        trs = []
+        for s in (1, 2, 3):
+            rid, pid, _ = topo.addr(others[s])
+            trs.append(RemoteDMATransfer(dst_ids=[DstId(rid=rid, pnc=pid)], dma_engine_mask=bits(masks[s]), remote_sem=sem[ar[s]],
+                                         src=R[:, s, c], dst=NX[:, s, c]))
+        op("G", 1000, lambda e: g.remote_dma_fused(trs, local_sem=sem.sent), sk[1:], [("mv", v, h, j)], sig=(None, 0))
+        op("E", 0, None, [("mv", v, h, j)], (), sig=("sent", sent * 2 * VI * NJ))
+        nk = [("ST", v + 1, h, j, s) for s in range(4)]
+        for s in (1, 2, 3):
+            op("E", 0, None, [("mv", v, h, j)], [nk[s]], lat=SEND_NS - 1500 * (s in near), sig=(ar[s], len(masks[s])))
+        if not last:
+            dma("Y", NX[:, 0, c], R[:, 0, c], ar[0], 16, sk[0:1], nk[0:1], 2200)
+            if ONECONV:
+                cp(U[:, 1:4, c], NX[:, 1:4, c], 3 * W, nk[1:], [("U", h, j, s) for s in (1, 2, 3)])
+            else:
+                for s in (2, 1, 3):
+                    cp(U[:, s, c], NX[:, s, c], W, [nk[s]], [("U", h, j, s)])
+        else:
+            for s in range(4):
+                for t in range(2):
+                    c0 = 256 * s + 128 * t + W * j
+                    dma("S" if (h and t) else "Y", T.ys[64 * h:64 * h + 64, c0:c0 + W], (NX if s else R)[64 * t:64 * t + 64, s, c],
+                        "out", 16 * (4 + 16 * NJ), [nk[s] if s else sk[0]], (), 2200)
+
+    for v in range(VI):
+        for h in range(2):
+            cur[0], cur[1] = 2 * v + h, 0
+            xr = [("X" if v else "Xl", h, t) for t in range(2)]
+            if v == 0:
+                cp(T["U%d" % h][:], T["ST0%d" % h][:], 512, [("STl", h, s, t) for s in range(4) for t in range(2)],
+                   [("U", h, j, s) for s in range(4) for j in range(NJ)] + [("ST", 0, h, j, s) for s in range(4) for j in range(NJ)])
+            cur[1] = 0
+            for j in range(2):
+                pairs_of_piece(v, h, j, xr)
+            for j in range(NJ):
+                cur[1] = 100 * (j + 1)
+                chunk(v, h, j, xr)
+    return ops
+
+
+ONECONV = False
+
+
+def schedule(ops):
+    if "order" not in PLAN:
+        pred = [sorted(o["deps"]) for o in ops]
+        succ = [[] for _ in ops]
+        for i, p in enumerate(pred):
+            for d in p:
+                succ[d].append(i)
+        for look, lead in TRIES:
+            prio = [0.0] * len(ops)
+            for o in reversed(ops):
+                prio[o["i"]] = o["dur"] + o["lat"] + 120 + max([prio[s] for s in succ[o["i"]]] + [0.0])
+            prio = [p + lead * (o["h"] == 0) for p, o in zip(prio, ops)]
+            for _ in range(8):
+                order, start, fin = place(ops, pred, succ, prio, look, False)
+                if max(fin) < PLAN.get("end", 1e18):
+                    PLAN.update({"order": order, "end": max(fin), "start": start})
+                prio = place(ops, succ, pred, fin, look, True)[2]
+    bank = {}
+    for i in PLAN["order"]:
+        o = ops[i]
+        o["t"] = PLAN["start"][i]
+        for b in o["banks"]:
+            for e2, d in bank.get(b, {}).items():
+                if e2 != o["eng"]:
+                    o["deps"].add(d)
+            bank.setdefault(b, {})[o["eng"]] = i
+    return PLAN["order"], PLAN["end"]
+
+
+PLAN = {}
+
+
+def place(ops, pred, succ, prio, look, back):
+    n = len(ops)
+    left = [len(p) for p in pred]
+    base, fin, start = [0.0] * n, [0.0] * n, [0.0] * n
+    free, bank, order, avail = {}, {}, [], {}
+    for i in range(n):
+        if not left[i]:
+            avail.setdefault(ops[i]["eng"], []).append(i)
+    while len(order) < n:
+        best = None
+        for e, l in avail.items():
+            if not l:
+                continue
+            c = []
+            for i in l:
+                t = max(base[i], free.get(e, 0.0))
+                for b in ops[i]["banks"]:
+                    for e2, d in bank.get(b, {}).items():
+                        if e2 != e:
+                            t = max(t, fin[d] + 130)
+                c.append((t, i))
+            t0 = min(c)[0]
+            if best is None or t0 < best[0]:
+                best = (t0, e, c)
+        t0, e, c = best
+        t, i = max([x for x in c if x[0] <= t0 + look], key=lambda x: prio[x[1]])
+        o = ops[i]
+        start[i] = t
+        for b in o["banks"]:
+            bank.setdefault(b, {})[e] = i
+        if e != "E":
+            free[e] = t + o["dur"]
+        fin[i] = t + o["dur"] + (0 if back else o["lat"])
+        order.append(i)
+        avail[e].remove(i)
+        for s in succ[i]:
+            e2 = ops[s]["eng"]
+            gap = 0 if (e if back else e2) in "DE" else 70 if e2 == e else 130
+            base[s] = max(base[s], fin[i] + gap + (ops[s]["lat"] if back else 0))
+            left[s] -= 1
+            if left[s] == 0:
+                avail.setdefault(e2, []).append(s)
+    return order, start, fin
+
+
+def rank_program(g, core, T, topo):
+    rank = T.rank_of(core)
+    if rank is None:
+        owner = [c for c in T.cores if core in helpers_of(c, T, topo)]
+        if not owner or not FOLD:
+            return
+        owner = owner[0]
+        hs = helpers_of(owner, T, topo)
+        ops = build(g, owner, T, topo)
+        order, _ = schedule(ops)
+        rid, pid, _ = topo.addr(owner)
+        ne, total = len(topo.engines(core, owner)), 0
+        for i in order:
+            tag = ops[i]["tag"]
+            if tag is None or hs[tag[2] % len(hs)] != core:
+                continue
+            v, h, f = tag
+            c0 = 2048 * PAIRS.index(FOLD[f][0:2]) + FOLD[f][2]
+            g.wait_ge(T.sem["ha%d%d" % (f, h)], (v + 1) * len(topo.engines(owner, core)))
+            g.remote_dma(T["M%d" % h][:, c0:c0 + FOLD[f][3]], helper_slot(T, v, h, f), T.sem["hb%d%d" % (f, h)],
+                         T.sem.hsent, pid, rid, topo.mask(core, owner))
+            total += ne
+        if total:
+            g.wait_ge(T.sem.hsent, total)
+        return
+    ops = build(g, core, T, topo)
+    order, _ = schedule(ops)
+    queue = {"V": g.vector, "S": g.scalar, "P": g.tensor, "G": g, "Y": g.sync}
+    needed = set()
+    for o in ops:
+        for d in o["deps"]:
+            if o["fn"] is not None and not (o["eng"] == "P" and ops[d]["eng"] == "P"):
+                needed.add(d)
+    count, waited, totals = {}, {}, {}
+    for i in order:
+        o = ops[i]
+        e = o["eng"]
+        mark = False
+        if o["sig"] is None:
+            if i in needed:
+                count[e] = count.get(e, 0) + 1
+                mark = True
+            o["sig"] = ("c" + e, count.get(e, 0))
+        if o["sig"][0] is not None:
+            totals[o["sig"][0]] = max(totals.get(o["sig"][0], 0), o["sig"][1])
+        if o["fn"] is None:
+            continue
+        want = {}
+        for d in o["deps"]:
+            s, val = ops[d]["sig"]
+            if s is None or (e == "P" and ops[d]["eng"] == "P"):
+                continue
+            want[s] = max(want.get(s, 0), val)
+        for s in sorted(want):
+            if want[s] > waited.get((e, s), 0):
+                queue[e].wait_ge(T.sem[s], want[s])
+                waited[(e, s)] = want[s]
+        ins = o["fn"](e)
+        if mark:
+            ins.then_inc(T.sem["c" + e], 1)
+    for s in sorted(totals):
+        if totals[s] > waited.get(("G", s), 0):
+            g.wait_ge(T.sem[s], totals[s])

@@ -4,56 +4,64 @@ from concourse.mybir import AluOpType, ActivationFunctionType
 A = AluOpType
 F = ActivationFunctionType
 VI = 5
-STAR = False
-NJ = 2
-W = 128 // NJ
-FOLD = [] if STAR else [(a, b, c, 1024) for c in (0, 1024) for a, b in ((0, 2), (0, 1), (1, 2))]
 PAIRS = [(0, 1), (2, 3), (0, 2), (1, 3), (0, 3), (1, 2)]
-SLOT = {0: 0, 2: 1, 1: 2}
-VGATHER = [(0, 0, 2, 0)]
-CY, GCY, SCAT, PECY, FIX = 1.04, 1.56, 3.8, 0.52, 60
-FOLD_NS, BACK_NS, SEND_NS = 4000, 2500, 5000
-TRIES = [(a, b) for a in (40, 60, 100, 150) for b in (0, 4000, 8000)]
+FOLD = [(a, b, c, 1024) for c in (0, 1024) for a, b in ((0, 2), (0, 1), (1, 2))]
+SP = 512
+MP = 512
+VGATHER = []
+VFIRST = [(2, 0), (2, 1), (2, 2), (2, 3)]
+TWIN_SCATTER = True
+JOIN = False
+OUTS = 16 * (4 + (16 if JOIN else 32))
+CY, GCY, SCAT, PECY, FIX, PFIX = 1.04, 1.56, 3.8, 0.52, 60, 5
+SAME, CROSS = 70, 130
+FOLD_NS, BACK_NS, SEND_NS, SEND_BUSY = 1850, 2800, 2500, 1300
+TRIES = [(a, b, c) for a in (20, 40, 80, 150) for b in (4000, 8000, 12000) for c in (3000, 6000, 10000, 15000)]
+ROUNDS = 4
 
 SCRATCH = {}
 for _h in range(2):
-    SCRATCH["X%d" % _h] = ("sbuf", [128, 4096], "bfloat16")
-    SCRATCH["P%d" % _h] = ("sbuf", [128, 4 * 2048], "bfloat16")
+    SCRATCH["X%d" % _h] = ("sbuf", [128, 4096 + 2048], "bfloat16")
+    SCRATCH["P%d" % _h] = ("sbuf", [128, 3 * 2048], "bfloat16")
     SCRATCH["M%d" % _h] = ("sbuf", [128, 6 * 2048], "bfloat16")
-    for _v in range(VI):
-        SCRATCH["ST%d%d" % (_v, _h)] = ("sbuf", [128, 4, 128], "int32")
-    SCRATCH["RF%d" % _h] = ("sbuf", [128, 4, 128], "float32")
-    SCRATCH["LF%d" % _h] = ("sbuf", [128, 4, 128], "float32")
+    SCRATCH["HI%d" % _h] = ("sbuf", [128, 4, 128], "int32")
+    SCRATCH["SC%d" % _h] = ("sbuf", [128, VI + 1, 7, 128], "float16")
+    SCRATCH["R%d" % _h] = ("sbuf", [128, VI, 4, 128], "float16")
+    SCRATCH["OF%d" % _h] = ("sbuf", [128, 4, 128], "float32")
     SCRATCH["U%d" % _h] = ("sbuf", [128, 4, 128], "uint16")
     SCRATCH["thi%d" % _h] = ("sbuf", [128, 4], "int32")
     SCRATCH["thr%d" % _h] = ("sbuf", [128, 4], "float32")
+    SCRATCH["MS%d" % _h] = ("sbuf", [128, 3, 128], "float16")
+    SCRATCH["fm%d" % _h] = ("sbuf", [128, 4, 128], "bfloat16")
+    SCRATCH["pT%d" % _h] = ("psum", [128, 512], "float32")
 for _n, _w, _d in [
-    ("bx", 128, "bfloat16"), ("sg", 128, "bfloat16"), ("cb", 128, "bfloat16"), ("at", 128, "bfloat16"),
-    ("acc", 4, "float32"), ("ai", 4, "int32"), ("ixp", 8, "uint16"), ("ixx", 8, "uint16"),
-    ("pb", 128, "bfloat16"), ("bs", 128, "bfloat16"), ("br", 128, "bfloat16"),
-    ("CI", 8, "int32"), ("CF", 8, "float32"), ("CX", 16, "float32"), ("J", 144, "float32"), ("JB", 128, "float32"),
-    ("JG", 128, "float32"), ("Wd", 144, "bfloat16"), ("NWd", 144, "bfloat16"), ("MI", 144, "bfloat16"),
-    ("ID", 640, "bfloat16"), ("bm", 8, "float32"), ("BC", 1024, "bfloat16"), ("AW", 128, "float32"),
-    ("eq", 8, "float32"), ("lam", 12, "float32"), ("WT", 512, "bfloat16"), ("RX", 384, "bfloat16"),
-    ("C256", 8, "bfloat16"), ("NEG", 128, "bfloat16"),
+    ("sg", 128, "bfloat16"), ("cb", 128, "bfloat16"), ("acc", 4, "float32"), ("ai", 4, "int32"), ("ix", 24, "uint16"),
+    ("bg", 256, "bfloat16"), ("br", 256, "bfloat16"), ("ov", 128, "float16"),
+    ("CI", 12, "int32"), ("CF", 12, "float32"), ("CX", 20, "float32"), ("J", 144, "float32"), ("JB", 128, "float32"),
+    ("JG", 128, "float32"), ("MI", 288, "bfloat16"), ("ID", 11 * 128, "bfloat16"), ("W37", 128, "float16"), ("WP", 512, "bfloat16"),
+    ("bm", 8, "bfloat16"), ("AW", 128, "float32"), ("eq", 8, "float32"), ("lam", 8, "float32"), ("WT", 7 * 128, "bfloat16"),
+    ("CK", 16, "float16"), ("CJ", 16, "float32"), ("NEG", 256, "bfloat16"), ("ONE", 128, "bfloat16"), ("ZE", 128, "bfloat16"),
+    ("RW", 64, "float32"), ("WS", 96, "bfloat16"),
 ]:
     SCRATCH[_n] = ("sbuf", [128, _w], _d)
-for _n, _w, _d in [("MS", 3, "float32"), ("LM", 3, "float16"), ("FM", 3, "float16"), ("ps", 3, "bfloat16"), ("sq", 3, "bfloat16"),
-                   ("DD", 2, "float32"), ("PR", 2, "int32"), ("WZ", 3, "float32"), ("WB", 11, "bfloat16")]:
+for _n, _w, _d in [("LM", 3, "float16"), ("FM", 2, "float16"), ("ps", 3, "bfloat16"), ("AT", 2, "bfloat16"),
+                   ("mm", 2, "float32"), ("PR", 2, "float32"), ("TI", 2, "int32"), ("HC", 2, "float16"), ("o2", 1, "float32"),
+                   ("WB", 21, "bfloat16")]:
     SCRATCH[_n] = ("sbuf", [128, _w, 128], _d)
+SCRATCH["CT"] = ("sbuf", [128, 2, 192], "float16")
 SCRATCH["SR"] = ("sbuf", [128, 3, 3], "float32")
 SCRATCH["AE"] = ("sbuf", [128, 3, 3, 12], "float32")
 SCRATCH["LH"] = ("sbuf", [128, 2, 3, 12], "float32")
 SCRATCH["LQ"] = ("sbuf", [128, 4, 3, 12], "float32")
-SCRATCH["AR"] = ("sbuf", [128, 11, 16], "float32")
-SCRATCH["pC"] = ("psum", [128, 2048 if STAR else 1536], "float32")
-for _n in ("pM", "pD", "pK", "pV") + (() if STAR else ("pO",)):
+SCRATCH["AR"] = ("sbuf", [128, 21, 16], "bfloat16")
+SCRATCH["pC"] = ("psum", [128, 1024], "float32")
+for _n in ("pA", "pD", "pE", "pK"):
     SCRATCH[_n] = ("psum", [128, 4, 128], "float32")
 
 SEMAPHORES = ["cV", "cS", "cP", "cG", "thl", "sent", "out", "hsent"]
 for _h in range(2):
-    SEMAPHORES += ["xl%d" % _h, "hl%d" % _h, "tw%d" % _h, "lf%d" % _h]
-    SEMAPHORES += ["ar%d%d%d%d" % (_v, _h, _j, _s) for _v in range(VI) for _j in range(NJ) for _s in range(4)]
+    SEMAPHORES += ["xl%d" % _h, "tw%d" % _h, "lf%d0" % _h, "lf%d1" % _h] + ["hl%d%d" % (_h, _s) for _s in range(4)]
+    SEMAPHORES += ["ar%d%d%d%d" % (_v, _h, _j, _s) for _v in range(VI) for _j in range(2) for _s in range(1, 4)]
     SEMAPHORES += ["ha%d%d" % (_f, _h) for _f in range(len(FOLD))] + ["hb%d%d" % (_f, _h) for _f in range(len(FOLD))]
 
 
@@ -70,19 +78,18 @@ def bits(engines):
 
 def helper_slot(T, v, h, f):
     n = (2 * v + h) * ((len(FOLD) + 2) // 3) + f // 3
-    name, j = [("P0", n), ("P1", n - 4), ("M0", n - 8), ("M1", n - 14)][0 if n < 4 else 1 if n < 8 else 2 if n < 14 else 3]
-    return T[name][:, j * 2048:j * 2048 + FOLD[f][3]]
+    name, j = [("M0", n), ("M1", n - 12), ("P0", n - 24), ("P1", n - 30)][0 if n < 12 else 1 if n < 24 else 2 if n < 30 else 3]
+    return T[name][:, j * 1024:j * 1024 + FOLD[f][3]]
 
 
 def build(g, core, T, topo):
-    ops, lastw, readers, cur = [], {}, {}, [-2, 0]
+    ops, lastw, readers, cur = [], {}, {}, [0]
     rank = T.rank_of(core)
     sem = T.sem
 
     def op(eng, dur, fn, r=(), w=(), banks=(), lat=0, sig=None, tag=None):
         o = {"eng": eng, "dur": dur, "fn": fn, "banks": banks, "lat": lat, "sig": sig, "deps": set(), "i": len(ops), "tag": tag,
-             "u": cur[0], "c": cur[1], "h": cur[0] % 2}
-        cur[1] += 1
+             "h": cur[0] % 2, "u": cur[0], "stop": False, "w": list(w)[0:2], "long": False}
         for k in r:
             if k in lastw:
                 o["deps"].update(lastw[k])
@@ -99,7 +106,7 @@ def build(g, core, T, topo):
         return o
 
     def vec(n, fn, r, w, banks=()):
-        return op("V", FIX + max(64, n) * CY, lambda e: fn(g.vector), r, w, banks)
+        return op("V", FIX + max(64, n) * CY, lambda o: fn(g.vector), r, w, banks)
 
     def ts(out, in0, s1, s2, o0, o1, n, r, w, banks=()):
         if o1 is None:
@@ -113,48 +120,53 @@ def build(g, core, T, topo):
         return vec(n, lambda q: q.tensor_copy(out, in_), r, w, banks)
 
     def act(out, in_, func, n, r, w, banks=(), **kw):
-        return op("S", FIX + 20 + max(64, n) * CY, lambda e: g.scalar.activation(out, in_, func, **kw), r, w, banks)
+        return op("S", FIX + 20 + max(64, n) * CY, lambda o: g.scalar.activation(out, in_, func, **kw), r, w, banks)
 
-    def pe(mms, r, w, banks):
-        def fn(e):
+    def pe(mms, r, w, banks, tag=None):
+        def fn(o):
             last = None
-            for m in mms:
-                last = g.tensor.matmul(m[0], m[1], m[2], m[3], m[4])
+            for i, m in enumerate(mms):
+                stop = m[4] if m[4] is not None else (o["stop"] and i == len(mms) - 1)
+                last = g.tensor.matmul(m[0], m[1], m[2], m[3], stop)
             return last
-        return op("P", sum([max(64, m[5]) * PECY + 5 for m in mms]), fn, r, w, banks, lat=60)
+        return op("P", sum([max(64, m[5]) * PECY + PFIX for m in mms]), fn, r, w, banks, lat=60, tag=tag)
 
-    def group(out, terms, n):
+    def group(out, terms, n=64):
         return [(out, a, b, i == 0, i == len(terms) - 1, n) for i, (a, b) in enumerate(terms)]
 
     def dma(eng, out, in_, s, total, r, w, lat):
         q = g.sync if eng == "Y" else g.scalar
-        return op(eng, 120, lambda e: q.dma_start(out, in_).then_inc(sem[s], 16), r, w, lat=lat, sig=(s, total))
+        return op(eng, 100, lambda o: q.dma_start(out, in_).then_inc(sem[s], 16), r, w, lat=lat, sig=(s, total))
 
     def iota(out, pattern, base, cm, w, n, flag=True):
         if flag:
-            return op("G", 160 + 2 * n * CY, lambda e: g.iota(out, pattern, base, cm, allow_small_or_imprecise_dtypes=True), (), w)
-        return op("G", 160 + 2 * n * CY, lambda e: g.iota(out, pattern, base, cm), (), w)
+            return op("G", 160 + 2 * n * CY, lambda o: g.iota(out, pattern, base, cm, allow_small_or_imprecise_dtypes=True), (), w)
+        return op("G", 160 + 2 * n * CY, lambda o: g.iota(out, pattern, base, cm), (), w)
 
     for h in range(2):
-        for s in range(4):
+        cur[0] = h
+        for s in (0, 2, 1, 3):
             for t in range(2):
-                dma("Y" if (h or t) else "S", T["ST0%d" % h][64 * t:64 * t + 64, s, :],
-                    T.hom[64 * h:64 * h + 64, 256 * s + 128 * t:256 * s + 128 * t + 128], "hl%d" % h, 128, (), [("STl", h, s, t)], 2200)
+                dma("Y" if (h or t) else "S", T["HI%d" % h][64 * t:64 * t + 64, s, :],
+                    T.hom[64 * h:64 * h + 64, 256 * s + 128 * t:256 * s + 128 * t + 128], "hl%d%d" % (h, s), 32, (), [("HI", h, s, t)], 2200)
             if s == 0:
                 for t in range(2):
-                    dma("Y" if (h or t) else "S", T["X%d" % h][64 * t:64 * t + 64, :], T.x[64 * h:64 * h + 64, :], "xl%d" % h, 32, (),
-                        [("Xl", h, t)], 4000)
-    CI, CF, CX, J, ID, AR, WB, BC = T.CI, T.CF, T.CX, T.J, T.ID, T.AR, T.WB, T.BC
+                    dma("Y" if (h or t) else "S", T["X%d" % h][64 * t:64 * t + 64, 0:4096], T.x[64 * h:64 * h + 64, :], "xl%d" % h, 32, (),
+                        [("Xl", h, t)], 4000 + 3500 * h)
+    cur[0] = 0
+    CI, CF, CX, J, ID, AR, WB, RW = T.CI, T.CF, T.CX, T.J, T.ID, T.AR, T.WB, T.RW
     iota(CI[:, 0:1], [[0, 1]], 0, 1, ["CI0"], 1, False)
     iota(J[:], [[1, 144]], 0, 0, ["J"], 144)
     iota(T.JB[:], [[16, 8], [0, 16]], 0, 0, ["JB"], 128)
     iota(T.AE[:, 0], [[0, 4], [1, 9]], 4, 0, ["AE0"], 36)
     iota(T.AE[:, 1], [[1, 4], [1, 9]], 5, 0, ["AE1"], 36)
-    iota(T.C256[:], [[256, 8]], 0, 0, ["C256"], 8)
+    iota(RW[:, 0:16], [[0, 2], [1, 8]], 0, 0, ["RW0"], 16)
+    iota(RW[:, 16:32], [[1, 2], [0, 8]], 0, 0, ["RW1"], 16)
+    iota(T.CJ[:], [[0, 2], [256, 8]], 4, 0, ["CJ"], 16)
     iota(T.JG[:], [[0, 2], [1, 4], [0, 16]], 0, 0, ["JG"], 128)
     for h in range(2):
         for t in range(2):
-            op("G", 600, lambda e, h=h, t=t: g.dma_start(T["thi%d" % h][64 * t:64 * t + 64, 0:1], T.th[64 * h:64 * h + 64, :],
+            op("G", 600, lambda o, h=h, t=t: g.dma_start(T["thi%d" % h][64 * t:64 * t + 64, 0:1], T.th[64 * h:64 * h + 64, :],
                                                           allow_slow_non_contiguous=True).then_inc(sem.thl, 16),
                (), [("thl", h, t)], lat=3000, sig=("thl", 64))
     q0 = CI[:, 0:1]
@@ -164,74 +176,107 @@ def build(g, core, T, topo):
     ts(CI[:, 4:5], q0, 112, None, A.bitwise_and, None, 1, ["CI0"], ["CI4"])
     ts(CI[:, 5:6], q0, 4, 3, A.arith_shift_right, A.bitwise_and, 1, ["CI0"], ["CI5"])
     ts(CI[:, 6:7], q0, 64, None, A.bitwise_and, None, 1, ["CI0"], ["CI6"])
-    cp(CF[:, 0:7], CI[:, 0:7], 7, ["CI%d" % i for i in range(7)], ["CF"])
-    qf, kf, Lf, Rf, bf, gf, tf = [CF[:, i:i + 1] for i in range(7)]
-    ts(T.Wd[:], J[:], 15.0, bf, A.subtract, A.is_equal, 144, ["J", "CF"], ["Wd"])
-    for i, c in enumerate((1.0, 2.0, 0.5, -0.5, -1.0)):
-        ts(ID[:, 128 * i:128 * i + 128], J[:, 0:128], qf, c, A.is_equal, A.mult, 128, ["J", "CF"], ["ID%d" % i])
-    I1, I2, IH, NIH, NI = [ID[:, 128 * i:128 * i + 128] for i in range(5)]
-    ts(T.NWd[:], T.Wd[:], -1.0, None, A.mult, None, 72, ["Wd"], ["NWd"])
-    ts(T.MI[:], T.Wd[:], kf, None, A.mult, None, 72, ["Wd", "CF"], ["MI"])
+    ts(CI[:, 7:8], q0, 3, 1, A.arith_shift_right, A.bitwise_and, 1, ["CI0"], ["CI7"])
+    ts(CI[:, 8:9], q0, 7, None, A.bitwise_and, None, 1, ["CI0"], ["CI8"])
+    cp(CF[:, 0:9], CI[:, 0:9], 9, ["CI%d" % i for i in range(9)], ["CF"])
+    qf, kf, Lf, Rf, bf, gf, tf, xf, jf = [CF[:, i:i + 1] for i in range(9)]
     ts(T.bm[:], T.JB[:, 0:128:16], bf, None, A.is_equal, None, 8, ["JB", "CF"], ["bm"])
+    vec(64, lambda q: q.memset(T.ZE[:], 0.0), (), ["ZE"])
+    vec(64, lambda q: q.memset(T.WS[:], 0.0), (), ["WS"])
+    for p in range(3):
+        ts(T.WS[:, 32 * p:32 * p + 8], T.bm[:], 2.0, None, A.mult, None, 8, ["bm", "WS"], ["WS%d" % p])
+        ts(T.WS[:, 72 + 8 * p:80 + 8 * p], T.bm[:], -1.0, None, A.mult, None, 8, ["bm", "WS"], ["WN%d" % p])
+    wsum = [T.WS[:, 24 * p:24 * p + 24] for p in range(4)]
+    wsk = [["WS0"], ["WS1"], ["WS2"], ["WN0", "WN1", "WN2"]]
+    cols = [(kf, 4.0, None, A.is_lt, None), (kf, 12.0, None, A.is_ge, None), (xf, 1024.0, -1024.0, A.mult, A.add), (xf, -1024.0, None, A.mult, None),
+            (jf, 4.0, None, A.add, None), (jf, 5.0, None, A.add, None), (xf, -2.0, 1.0, A.mult, A.add), (xf, 2.0, -1.0, A.mult, A.add),
+            (xf, -1.0, None, A.add, None), (kf, -4.0, None, A.add, None), (kf, 1184.0, None, A.mult, None), (tf, -32.0, 4096.0, A.mult, A.add),
+            (tf, -2.0, 64.0, A.mult, A.add), (kf, 16.0, None, A.mult, None)]
+    for i, c in enumerate(cols):
+        ts(CX[:, i:i + 1], c[0], c[1], c[2], c[3], c[4], 1, ["CF"], ["CX%d" % i])
+    cx = [CX[:, i:i + 1] for i in range(20)]
+    ts(cx[14], cx[12], qf, None, A.add, None, 1, ["CX12", "CF"], ["CX14"])
+    ts(cx[12], cx[12], bf, None, A.add, None, 1, ["CX14", "CF"], ["CX12"])
+    ts(cx[15], jf, 1.0, cx[8], A.add, A.mult, 1, ["CF", "CX8"], ["CX15"])
+    I1, NI, I32, I4096, I2048, IOFF, SW, N32, PMT, PM, NPM = [ID[:, 128 * i:128 * i + 128] for i in range(11)]
+    ts(I1, J[:, 0:128], qf, None, A.is_equal, None, 128, ["J", "CF"], ["ID0"])
+    for i, c in ((1, -1.0), (2, 32.0), (3, 4096.0), (4, 2048.0), (5, -127.0 * 65536), (7, -32.0)):
+        act(ID[:, 128 * i:128 * i + 128], I1, F.Copy, 128, ["ID0"], ["ID%d" % i], scale=c)
+    ts(SW, J[:, 0:128], cx[14], None, A.is_equal, None, 128, ["J", "CX14"], ["ID6"])
+    W37 = T.W37[:]
+    ts(W37, I1, cx[10], None, A.mult, None, 128, ["ID0", "CX10"], ["W37"])
+    ts(cx[16], xf, 64.0, jf, A.mult, A.add, 1, ["CF"], ["CX16"])
+    ts(cx[17], bf, 0.5, cx[16], A.mult, A.add, 1, ["CF", "CX16"], ["CX17"])
+    ts(PMT, J[:, 0:128], cx[17], None, A.is_equal, None, 128, ["J", "CX17"], ["PMT"])
+    for i, c in enumerate((bf, cx[12])):
+        ts(T.MI[:, 144 * i:144 * i + 144], J[:], 15.0, c, A.subtract, A.is_equal, 144, ["J", "CF", "CX12"], ["MI%d" % i])
+        ts(T.MI[:, 144 * i:144 * i + 144], T.MI[:, 144 * i:144 * i + 144], cx[15], -1.0, A.mult, A.mult, 72, ["CX15"], ["MI%d" % i])
+    ts(T.CJ[:], T.CJ[:], cx[13], None, A.add, None, 16, ["CX13"], ["CJ"])
+    ts(T.CK[:, 0:8], T.CJ[:, 0:8], cx[11], 4096.0, A.subtract, A.add, 8, ["CJ", "CX11"], ["CK0"])
+    ts(T.CK[:, 8:16], T.CJ[:, 8:16], cx[11], -2048.0, A.add, A.add, 8, ["CJ", "CX11"], ["CK1"])
     eq, lam = T.eq, T.lam
     ts(eq[:, 0:3], J[:, 0:3], Lf, None, A.is_equal, None, 3, ["J", "CF"], ["eqL"])
     ts(eq[:, 4:7], J[:, 0:3], Rf, None, A.is_equal, None, 3, ["J", "CF"], ["eqR"])
     tt(lam[:, 0:3], eq[:, 0:3], eq[:, 4:7], A.subtract, 3, ["eqL", "eqR"], ["lam"])
-    tt(lam[:, 8:11], lam[:, 0:3], lam[:, 0:3], A.mult, 3, ["lam"], ["lam2"])
-    ts(lam[:, 8:11], lam[:, 8:11], 0.5, None, A.mult, None, 3, ["lam2"], ["lam2"])
-    tt(lam[:, 4:7], lam[:, 8:11], eq[:, 0:3], A.add, 3, ["lam2", "eqL"], ["Fc"])
-    ts(lam[:, 5:6], lam[:, 4:5], lam[:, 6:7], -1.0, A.add, A.mult, 1, ["Fc"], ["Fc1"])
-    ts(lam[:, 5:6], lam[:, 5:6], 1.0, None, A.add, None, 1, ["Fc1"], ["Fc1"])
+    tt(lam[:, 4:7], eq[:, 4:7], eq[:, 0:3], A.subtract, 3, ["eqL", "eqR"], ["nlam"])
     tt(lam[:, 3:4], Lf, Rf, A.not_equal, 1, ["CF"], ["sw"])
-    ts(lam[:, 7:8], lam[:, 3:4], -0.5, None, A.mult, None, 1, ["sw"], ["Wc"])
-    for i in range(8):
-        ts(BC[:, 128 * i:128 * i + 128], T.JB[:], bf, lam[:, i:i + 1], A.is_equal, A.mult, 128,
-           ["JB", "CF", "lam", "sw", "Fc", "Fc1", "Wc"], ["BC%d" % i])
-    bc = [BC[:, 128 * i:128 * i + 128] for i in range(8)]
-    bck = ["BC%d" % i for i in range(8)]
-    ts(T.AW[:], T.JG[:], gf, lam[:, 3:4], A.is_equal, A.mult, 128, ["JG", "CF", "sw"], ["AW"])
-    ts(CX[:, 0:1], kf, 4.0, None, A.is_lt, None, 1, ["CF"], ["CX0"])
-    ts(CX[:, 1:2], kf, 12.0, None, A.is_ge, None, 1, ["CF"], ["CX1"])
-    ts(CX[:, 2:3], kf, 16.0, None, A.mult, None, 1, ["CF"], ["CX2"])
-    ts(CX[:, 3:4], tf, 32.0, CX[:, 2:3], A.mult, A.add, 1, ["CF", "CX2"], ["CX3"])
-    ts(CX[:, 4:5], kf, 37.0, None, A.mult, None, 1, ["CF"], ["CX4"])
+    sw = lam[:, 3:4]
+    ts(T.AW[:], T.JG[:], gf, sw, A.is_equal, A.mult, 128, ["JG", "CF", "sw"], ["AW"])
     vec(88, lambda q: q.memset(AR[:], 0.0), (), ["AR"])
-    vec(64, lambda q: q.memset(T.NEG[:], -128.0), (), ["NEG"])
+    vec(128, lambda q: q.memset(T.NEG[:], -128.0), (), ["NEG"])
+    vec(64, lambda q: q.memset(T.ONE[:], 1.0), (), ["ONE"])
     SR = T.SR
     vec(9, lambda q: q.memset(SR[:], 0.0), (), ["SR"])
     for i, (a, c) in enumerate(((SR[:, 0, 0:2], -1.0), (SR[:, 1, 2:3], -1.0), (SR[:, 1, 0:1], 1.0), (SR[:, 2, 1:3], 1.0))):
         vec(2, lambda q, a=a, c=c: q.memset(a, c), ["SR"], ["SR%d" % i])
     srk = ["SR0", "SR1", "SR2", "SR3", "AR"]
-    ts(AR[:, 0:3, 0:3], SR[:], CX[:, 0:1], None, A.mult, None, 9, srk + ["CX0"], ["AR0"])
-    ts(AR[:, 0:3, 3:6], SR[:], CX[:, 1:2], None, A.mult, None, 9, srk + ["CX1"], ["AR1"])
+    ark = []
+
+    def ar(fn, out, *args):
+        ark.append("AR%d" % len(ark))
+        fn(out, *(args[:-1] + (args[-1] + ["AR"], [ark[-1]])))
+    ar(ts, AR[:, 0:3, 0:3], SR[:], cx[0], None, A.mult, None, 9, srk + ["CX0"])
+    ar(ts, AR[:, 0:3, 3:6], SR[:], cx[1], None, A.mult, None, 9, srk + ["CX1"])
+    ar(ts, AR[:, 15:18, 0:3], SR[:], cx[2], None, A.mult, None, 9, srk + ["CX2"])
+    ar(ts, AR[:, 15:18, 3:6], SR[:], cx[3], None, A.mult, None, 9, srk + ["CX3"])
     AE, LH, LQ = T.AE, T.LH, T.LQ
     ts(AE[:, 2], AE[:, 1], 13.0, -9.0, A.is_ge, A.mult, 36, ["AE1"], ["AE2"])
     tt(AE[:, 2], AE[:, 2], AE[:, 1], A.add, 72, ["AE1", "AE2"], ["AE2"])
     tt(LH[:, 0], AE[:, 0], AE[:, 2], A.min, 72, ["AE0", "AE2"], ["LH0"])
     tt(LH[:, 1], AE[:, 0], AE[:, 2], A.max, 72, ["AE0", "AE2"], ["LH1"])
     for i in range(2):
-        ts(LQ[:, i], LH[:, i], kf, None, A.is_le, None, 36, ["LH%d" % i, "CF"], ["LQ%d" % i])
-        ts(LQ[:, 2 + i], LH[:, i], kf, None, A.is_equal, None, 36, ["LH%d" % i, "CF"], ["LQ%d" % (2 + i)])
-    tt(AR[:, 3:6, 0:12], LQ[:, 0], LQ[:, 1], A.subtract, 72, ["LQ0", "LQ1", "AR"], ["AR2"])
-    tt(AR[:, 6:9, 0:12], LQ[:, 2], LQ[:, 3], A.subtract, 72, ["LQ2", "LQ3", "AR"], ["AR3"])
+        ts(LQ[:, i], LH[:, i], cx[4], cx[6], A.is_le, A.mult, 36, ["LH%d" % i, "CX4", "CX6"], ["LQ%d" % i])
+        ts(LQ[:, 2 + i], LH[:, i], cx[5], 2.0, A.is_equal, A.mult, 36, ["LH%d" % i, "CX5"], ["LQ%d" % (2 + i)])
+    ar(tt, AR[:, 3:6, 0:12], LQ[:, 0], LQ[:, 1], A.subtract, 72, ["LQ0", "LQ1"])
+    ar(tt, AR[:, 18:21, 0:12], LQ[:, 2], LQ[:, 3], A.subtract, 72, ["LQ2", "LQ3"])
     for i in range(2):
         c = 4 * i
-        ts(AR[:, 9, 3 * i:3 * i + 2], eq[:, c + 1:c + 3], eq[:, c:c + 1], -1.0, A.subtract, A.mult, 2, ["eqL", "eqR", "AR"], ["AR4%d" % i])
-        tt(AR[:, 9, 3 * i + 2:3 * i + 3], eq[:, c + 1:c + 2], eq[:, c + 2:c + 3], A.subtract, 2, ["eqL", "eqR", "AR"], ["AR5%d" % i])
-    ts(AR[:, 10, :], J[:, 0:16], kf, None, A.is_ge, None, 16, ["J", "CF", "AR"], ["AR6"])
-    ark = ["AR0", "AR1", "AR2", "AR3", "AR40", "AR41", "AR50", "AR51", "AR6", "bm"]
+        ar(ts, AR[:, 14, 3 * i:3 * i + 2], eq[:, c + 1:c + 3], eq[:, c:c + 1], -1.0, A.subtract, A.mult, 2, ["eqL", "eqR"])
+        ar(tt, AR[:, 14, 3 * i + 2:3 * i + 3], eq[:, c + 1:c + 2], eq[:, c + 2:c + 3], A.subtract, 2, ["eqL", "eqR"])
+    ar(ts, AR[:, 6, :], RW[:, 0:16], cx[9], None, A.is_equal, None, 16, ["RW0", "CX9"])
+    ts(RW[:, 32:48], J[:, 0:16], 4.0, None, A.is_ge, None, 16, ["J"], ["RW2"])
+    for i in range(2):
+        ar(ts, AR[:, 7 + i, :], RW[:, 16:32], lam[:, 2 * i:2 * i + 1], sw, A.mult, A.add, 16, ["RW1", "lam", "sw"])
+        ar(ts, AR[:, 9 + i, 4:16], J[:, 4:16], cx[5], cx[7 + i], A.is_lt, A.mult, 16, ["J", "CX5", "CX7", "CX8"])
+        ar(ts, AR[:, 11 + i, :], RW[:, 32:48], lam[:, 4 + 2 * i:5 + 2 * i], eq[:, 2 * i:2 * i + 1], A.mult, A.add, 16, ["RW2", "nlam", "eqL"])
+    ar(ts, AR[:, 13, :], RW[:, 32:48], sw, None, A.mult, None, 16, ["RW2", "sw"])
     for b in range(8):
-        ts(WB[:, :, 16 * b:16 * b + 16], AR[:], T.bm[:, b:b + 1], None, A.mult, None, 176, ark, ["WB%d" % b])
+        ts(WB[:, :, 16 * b:16 * b + 16], AR[:], T.bm[:, b:b + 1], None, A.mult, None, 168, ark + ["bm"], ["WB%d" % b])
     wbk = ["WB%d" % b for b in range(8)]
-    pD, pM, pK, pV, pC = T.pD, T.pM, T.pK, T.pV, T.pC
-    cp(T.WZ[:], WB[:, 0:3, :], 384, wbk, ["WZ"])
-    alld = [("D", i, j) for i in range(4) for j in range(NJ)]
-    pe([(pD[:, j, :], WB[:, 6 + j, :], I1, True, True, 128) for j in range(4)], wbk + ["ID0"], alld, ["D"])
-    act(T.WT[:], pD[:], F.Copy, 512, alld, ["WT"], ["D"])
-    RT = WB[:, 10, :]
-    for i, c in enumerate((0.5, -1.0, -0.5)):
-        ts(T.RX[:, 128 * i:128 * i + 128], RT, c, None, A.mult, None, 64, wbk, ["RX%d" % i])
-    RTH, NRT, NRTH = [T.RX[:, 128 * i:128 * i + 128] for i in range(3)]
+    pA, pD, pE, pK, pC = T.pA, T.pD, T.pE, T.pK, T.pC
+    ak, dk, ek = [[(n, j, i) for j in range(2) for i in range(4)] for n in "ADE"]
+    pe([(pE[:, i, :], PMT, WB[:, w, :], True, True, 128) for i, w in enumerate((0, 1, 2, 6))], wbk + ["PMT"], ek, ["E"])
+    act(T.WP[:], pE[:], F.Copy, 512, ek, ["WP"], ["E"])
+    wp = [T.WP[:, 128 * i:128 * i + 128] for i in range(4)]
+    pe([(pK[:, 0, :], PMT, I1, True, True, 128)], ["PMT", "ID0"], [("K", 0, 0), ("K", 1, 0)], ["K"])
+    act(PM, pK[:, 0, :], F.Copy, 128, [("K", 0, 0), ("K", 1, 0)], ["PM"], ["K"])
+    act(NPM, pK[:, 0, :], F.Copy, 128, [("K", 0, 0), ("K", 1, 0)], ["NPM"], ["K"], scale=-1.0)
+    pe([(pD[:, j, :], WB[:, 14 + j, :], I1, True, True, 128) for j in range(4)], wbk + ["ID0"], dk, ["D"])
+    pe([(pA[:, j, :], WB[:, 18 + j, :], I1, True, True, 128) for j in range(3)], wbk + ["ID0"], ak + [("Ax", 0), ("Ax", 1), "Aa"], ["A"])
+    act(T.WT[:, 0:512], pD[:], F.Copy, 512, dk, ["WT0"], ["D"])
+    act(T.WT[:, 512:896], pA[:, 0:3, :], F.Copy, 384, ak, ["WT1"], ["A"])
+    wt = [T.WT[:, 128 * i:128 * i + 128] for i in range(7)]
+    wb = [WB[:, i, :] for i in range(14)]
     for h in range(2):
         cp(T["thr%d" % h][:, 0:1], T["thi%d" % h][:, 0:1], 1, [("thl", a, b) for a in range(2) for b in range(2)], [("thr", h)])
 
@@ -241,9 +286,8 @@ def build(g, core, T, topo):
     masks, used = {}, []
     for i, s in enumerate(far):
         e = topo.engines(core, others[s])
-        e = e[i * len(e) // len(far):(i + 1) * len(e) // len(far)]
-        masks[s] = e
-        used += e
+        masks[s] = e[i * len(e) // len(far):(i + 1) * len(e) // len(far)]
+        used += masks[s]
     near = [s for s in (1, 2, 3) if s not in far]
     for i, s in enumerate(near):
         e = [x for x in topo.engines(core, others[s]) if x not in used]
@@ -251,211 +295,236 @@ def build(g, core, T, topo):
     sent = sum([len(masks[s]) for s in (1, 2, 3)])
     crot = [0]
 
-    def pairs_of_piece(v, h, j, xr):
-        X, P, M, U = T["X%d" % h], T["P%d" % h], T["M%d" % h], T["U%d" % h]
-        jc, lo = j * NJ // 2, 1024 * j
+    def costs(v, h, j, xr):
+        X, P, M, U, pT = T["X%d" % h], T["P%d" % h], T["M%d" % h], T["U%d" % h], T["pT%d" % j]
+        bank, lo, mine = ["T%d" % j], 1024 * j, (2 * j, 2 * j + 1)
+        first = len(ops)
+
+        def ps(s, a, b, step=1):
+            return X[:, 4096 + a:4096 + b:step] if s == 0 else P[:, 2048 * (s - 1) + a:2048 * (s - 1) + b:step]
+
+        def add_sums(tile, w, r, name):
+            pe([(pT[:, k:192:8], tile(k), wsum[w], False, None, 64) for k in range(8)], r + wsk[w] + [("Tz", j)], [("Ts", j, name)], bank,
+               tag=("acc", v, h, j))
+        pe([(pT[:, 0:192], T.ZE[:], ID[:, 0:192], True, False, 192)], ["ZE", "ID0", "ID1"], [("Tz", j)], bank)
+        onv = VFIRST if (v, h) == (0, 0) else VGATHER
         for s in (0, 2, 1, 3):
-            out = P[:, 2048 * s + lo:2048 * s + lo + 1024]
-            win = X[:, 0:4096].indirect(U[:, s, 64 * j:64 * j + 64])
-            rk = xr + [("U", h, jc, s)]
-            if STAR and s:
-                tt(out, win, P[:, lo:lo + 1024], A.subtract, 1024 * GCY, rk + [("P", h, 0, j)], [("P", h, s, j)])
-                pi = PAIRS.index((0, s))
-                act(M[:, 2048 * pi + lo:2048 * pi + lo + 1024], out, F.Abs, 1024, [("P", h, s, j)], [("M", h, pi, j)])
-            elif (v, h, s, j) in VGATHER:
-                cp(out, win, 1024 * GCY, rk, [("P", h, s, j)])
-            else:
-                act(out, win, F.Copy, 1024 * GCY, rk, [("P", h, s, j)])
-        for f, (a, b, c0, n) in enumerate(FOLD):
-            if (c0 + n - 1) // 1024 != j:
-                continue
+            whole = SP == 1024 and not [q for q in mine if (s, q) in onv]
+            for q, n in ([(mine[0], 2)] if whole else [(q, 1) for q in mine]):
+                win = X[:, 0:4096].indirect(U[:, s, 32 * q:32 * (q + n)])
+                rk, wk = xr + [("U", h, j, s)], [("P", h, s, q + i) for i in range(n)]
+                if (s, q) in onv:
+                    cp(ps(s, 512 * q, 512 * (q + n)), win, 512 * n * GCY, rk, wk)
+                else:
+                    act(ps(s, 512 * q, 512 * (q + n)), win, F.Copy, 512 * n * GCY, rk, wk)
+            add_sums(lambda k, s=s: ps(s, lo + k, lo + 1024, 8), 3, [("P", h, s, q) for q in mine], s)
+        folds = [f for f in range(len(FOLD)) if FOLD[f][2] // 1024 == j]
+        for f in folds:
+            a, b, c0, n = FOLD[f]
             hc = helpers[f % len(helpers)]
             rid, pid, _ = topo.addr(hc)
             pi = PAIRS.index((a, b))
-            js = range(c0 // 1024, (c0 + n) // 1024)
-            pk = [("P", h, s, i) for s in (a, b) for i in js]
-            mk = [("M", h, pi, i) for i in js]
+            qs = range(c0 // 512, (c0 + n) // 512)
+            pk = [("P", h, s, q) for s in (a, b) for q in qs]
+            mk = [("M", h, pi, q) for q in qs]
+            lf = "lf%d%d" % (h, j)
             tr = RemoteDMATransfer(dst_ids=[DstId(rid=rid, pnc=pid)], dma_engine_mask=topo.mask(core, hc), remote_sem=sem["ha%d%d" % (f, h)],
-                                   srcs=[P[:, 2048 * a + c0:2048 * a + c0 + n], P[:, 2048 * b + c0:2048 * b + c0 + n]],
-                                   dsts=[helper_slot(T, v, h, f)], alu_op=2)
-            op("G", 1000, lambda e, tr=tr: g.remote_dma_fused([tr], local_sem=sem["lf%d" % h]), pk, mk + [("f1", v, h, f)],
-               sig=(None, 0), tag=(v, h, f))
-            op("D", FOLD_NS * n / 2048, None, pk + [("f1", v, h, f)], [("f2", v, h, f)],
-               sig=("lf%d" % h, (v + 1) * len(topo.engines(core, hc)) * len(FOLD)))
-            op("E", 0, None, [("f2", v, h, f)], mk, lat=BACK_NS + FOLD_NS * n / 4096,
+                                   srcs=[ps(a, c0, c0 + n), ps(b, c0, c0 + n)], dsts=[helper_slot(T, v, h, f)], alu_op=2)
+            op("G", 700, lambda o, tr=tr, lf=lf: g.remote_dma_fused([tr], local_sem=sem[lf]), pk, mk + [("f1", v, h, f)],
+               sig=(None, 0), tag=("fold", v, h, f))
+            op("D", FOLD_NS * n / 1024, None, pk + [("f1", v, h, f)], [("f2", v, h, f)],
+               sig=(lf, (v + 1) * len(topo.engines(core, hc)) * len(folds)))
+            op("E", 0, None, [("f2", v, h, f)], mk, lat=BACK_NS + FOLD_NS * n / 2048,
                sig=("hb%d%d" % (f, h), (v + 1) * len(topo.engines(hc, core))))
-        if STAR:
-            for a, b in ((1, 2), (2, 3), (1, 3)):
-                pi = PAIRS.index((a, b))
-                base = 1024 * (crot[0] % 2)
-                bk = ["C%d" % (base // 512), "C%d" % (base // 512 + 1)]
+        for q in (mine if MP == 512 else mine[0:1]):
+            c0, qs = 512 * q, range(q, q + MP // 512)
+            for b in range(1, 4):
+                todo = [a for a in range(b) if not [x for x in FOLD if x[0:2] == (a, b) and x[2] <= c0 < x[2] + x[3]]]
+                if not todo:
+                    continue
                 crot[0] += 1
-                mm = []
-                for i in (0, 512):
-                    mm += group(pC[:, base + i:base + i + 512], [(I1, P[:, 2048 * a + lo + i:2048 * a + lo + i + 512]),
-                                                                 (NI, P[:, 2048 * b + lo + i:2048 * b + lo + i + 512])], 512)
-                pe(mm, [("P", h, a, j), ("P", h, b, j), "ID0", "ID4"], bk, bk)
-                act(M[:, 2048 * pi + lo:2048 * pi + lo + 1024], pC[:, base:base + 1024], F.Abs, 1024, bk, [("M", h, pi, j)], bk)
-        for b in range(1, 4):
-            mine = [a for a in range(b) if not [x for x in FOLD if x[0:2] == (a, b) and x[2] <= lo < x[2] + x[3]]]
-            if not mine or STAR:
-                continue
-            crot[0] += 1
-            for c0, n, base, bk in ([(lo, 1024, 0, ["C0", "C1"])] if crot[0] % 2 else [(lo, 512, 1024, ["C2"]), (lo + 512, 512, 0, ["C0"])]):
-                pe([(pC[:, base + i:base + i + 512], I1, P[:, 2048 * b + c0 + i:2048 * b + c0 + i + 512], True, True, 512)
-                    for i in range(0, n, 512)], [("P", h, b, j), "ID0"], bk, bk)
-                for a in mine:
+                base, bk = (512 * (crot[0] % 2), ["C%d" % (crot[0] % 2)]) if MP == 512 else (0, ["C0", "C1"])
+                pe([(pC[:, base + i:base + i + 512], I1, ps(b, c0 + i, c0 + i + 512), True, True, 512) for i in range(0, MP, 512)],
+                   [("P", h, b, x) for x in qs] + ["ID0"], bk, bk)
+                for a in todo:
                     pi = PAIRS.index((a, b))
-                    tt(M[:, 2048 * pi + c0:2048 * pi + c0 + n], pC[:, base:base + n], P[:, 2048 * a + c0:2048 * a + c0 + n],
-                       A.max, n, bk + [("P", h, a, j)], [("M", h, pi, j)], bk)
-        for p in range(3):
-            terms = [(T.Wd[:, 15 - k:143 - k], M[:, 2048 * pi + lo + k:2048 * pi + lo + 1024:16])
-                     for pi in (2 * p, 2 * p + 1) for k in range(16)]
-            pe(group(pM[:, SLOT[p], 64 * j:64 * j + 64], terms, 64), [("M", h, 2 * p, j), ("M", h, 2 * p + 1, j), "Wd"], [("pM", p, j)], ["M"])
+                    tt(M[:, 2048 * pi + c0:2048 * pi + c0 + MP], pC[:, base:base + MP], ps(a, c0, c0 + MP),
+                       A.max, MP, bk + [("P", h, a, x) for x in qs], [("M", h, pi, x) for x in qs], bk)
+        for pi in range(6):
+            add_sums(lambda k, pi=pi: M[:, 2048 * pi + lo + k:2048 * pi + lo + 1024:8], pi // 2, [("M", h, pi, q) for q in mine], 4 + pi)
+        for o in ops[first:]:
+            o["long"] = o["eng"] in "SVP"
 
-    def chunk(v, h, j, xr):
-        X, P, U, ST = T["X%d" % h], T["P%d" % h], T["U%d" % h], T["ST%d%d" % (v, h)]
-        last = v == VI - 1
-        c = slice(W * j, W * j + W)
-        ci = slice(W // 16 * j, W // 16 * (j + 1))
-        pieces = range(2 * j // NJ, 2 * (j + 1) // NJ)
-        thr = T["thr%d" % h][:, 0:1]
-        sk = [("ST", v, h, j, s) for s in range(4)]
-        dk = [("D", i, j) for i in range(4)]
-        pO, OB = (pM[:, 3, c], "M") if STAR else (T.pO[:, 0, c], "O")
+    def decide(v, h, j):
+        pT, fm = T["pT%d" % j], T["fm%d" % h]
+        c = slice(64 * j, 64 * j + 64)
+        CT = T.CT[:, j, :]
+        MS, LM, AT, cb, sg = T["MS%d" % h], T.LM, T.AT, T.cb[:, c], T.sg[:, c]
+        ak, dk = [[(n, j, i) for i in range(4)] for n in "AD"]
+        ms = ("MS", h, j)
 
         def k(name):
             return (name, j)
-        for i, s in enumerate(() if STAR else (0, 2, 1, 3)):
-            pe([(pO, T.NWd[:, 15 - r:143 - r], P[:, 2048 * s + 16 * W * j + r:2048 * s + 16 * W * (j + 1):16], i == 0 and r == 0, False, W)
-                for r in range(16)], [("P", h, s, q) for q in pieces] + ["NWd"], ["O"], [OB])
-        MS, cb, at = T.MS[:, :, c], T.cb[:, c], T.at[:, c]
-        act(MS, pM[:, 0:3, c], F.Copy, 3 * W, [("pM", p, q) for p in range(3) for q in pieces], [k("MS")], ["M"])
-        d = [pD[:, i, c] for i in range(4)]
-        d3 = pD[:, 0:3, c]
-        pe(group(d[0], [(T.WZ[:, p, :], T.MS[:, SLOT[p], c]) for p in range(3)], 4 * W), ["WZ", k("MS")], dk[0:1], ["D"])
-        act(T.sg[:, c], d[0], F.Sign, W, dk[0:1], [k("sg")], ["D"], bias=0.5)
-        pe(group(d[3], [(T.WT[:, 384:512], T.sg[:, c])], W), ["WT", k("sg")], dk[3:], ["D"])
-        act(cb, d[3], F.Relu, W + 130, dk[3:], [k("cb"), k("acc")], ["D"], bias=-3.0, accum_out=T.acc[:, j:j + 1])
-        pe([(d[SLOT[p]], bc[p], cb, True, True, W) for p in range(3)], bck + [k("cb")], dk[0:3], ["D"])
-        tt(T.LM[:, :, c], d3, MS, A.mult, 3 * W, dk[0:3] + [k("MS")], [k("LM")], ["D"])
+        cp(CT, pT[:, 0:192], 192, [("Ts", j, n) for n in range(10)] + [("Tz", j)], [k("CT")], ["T%d" % j])
+        pe([(pA[64 * x:64 * x + 64, p, c], T.CT[:, j, 64 * p:64 * p + 64], ID[:, x:128:2], True, True, 64) for p in range(3) for x in range(2)],
+           [k("CT"), "ID0"], ak[0:3], ["A"])
+        cp(MS[:, :, c], pA[:, 0:3, c], 192, ak[0:3], [ms], ["A"])
+        pe(group(pD[:, 0, c], [(wp[p], MS[:, p, c]) for p in range(3)]), ["WP", ms], dk[0:1], ["D"])
+        act(sg, pD[:, 0, c], F.Sign, 64, dk[0:1], [k("sg")], ["D"], bias=0.5)
+        mm = []
+        for p in range(3):
+            mm += group(pA[:, p, c], [(wp[3], MS[:, p, c]), (wt[1 + p], sg)])
+        pe(mm, ["WP", "WT0", ms, k("sg")], ak[0:3], ["A"])
+        pe(group(pD[:, 3, c], [(wt[0], sg)]), ["WT0", k("sg")], dk[3:], ["D"])
+        ts(LM[:, :, c], pA[:, 0:3, c], -2048.0, 0.0, A.add, A.max, 192, ak[0:3], [k("LM")], ["A"])
+        act(cb, pD[:, 3, c], F.Relu, 84, dk[3:], [k("cb"), k("acc")], ["D"], bias=-3.0, accum_out=T.acc[:, j:j + 1])
         mm = []
         for q in range(3):
-            mm += group(d[q], [(WB[:, 3 + q, :], T.LM[:, i, c]) for i in range(3)], W)
+            mm += group(pD[:, q, c], [(wb[3 + q], LM[:, p, c]) for p in range(3)])
         pe(mm, wbk + [k("LM")], dk[0:3], ["D"])
-        act(T.ps[:, :, c], d3, F.Sign, 3 * W, dk[0:3], [k("ps")], ["D"], bias=0.5)
-        pe(group(d[3], [(T.WT[:, 128 * q:128 * q + 128], T.ps[:, q, c]) for q in range(3)], W), ["WT", k("ps")], dk[3:], ["D"])
-        act(at, d[3], F.Relu, W, dk[3:], [k("at")], ["D"], bias=-7.0)
-        ix = pD[:, 3, W * j:W * j + W // 16]
-        pe(group(ix, [(T.MI[:, 15 - r:143 - r], T.at[:, W * j + r:W * j + W:16]) for r in range(16)] + [(I1, T.C256[:, ci])], 64),
-           ["MI", k("at"), "ID0", "C256"], dk[3:], ["D"])
-        ts(T.ixp[:, ci], ix, CX[:, 2:3], None, A.add, None, 8, dk[3:] + ["CX2"], [k("ixp")], ["D"])
-        ts(T.ixx[:, ci], ix, CX[:, 3:4], None, A.add, None, 8, dk[3:] + ["CX3"], [k("ixx")], ["D"])
-        if j == NJ - 1:
-            js = range(NJ)
-            act(T.pb[:], P[:, 0:2048].indirect(T.ixp[:]), F.Copy, 128 * GCY, [("P", h, 0, 0), ("P", h, 0, 1)] + [("ixp", q) for q in js], ["pb"])
-            xk, ik = [("X", h, 0), ("X", h, 1)], [("ixx", q) for q in js]
-            tt(T.bs[:], X[:, 0:4096].indirect(T.ixx[:]), T.pb[:], A.add, 128 * GCY, xr + ik + ["pb"], ["bs"])
-            act(T.br[:], T.bs[:], F.Identity, 128, ["bs"], ["br"], scale=0.5, bias=127.8)
-            tt(X[:, 0:4096].indirect(T.ixx[:]), T.br[:], T.NEG[:], A.add, 128 * SCAT, ["br", "NEG"] + ik, xk + (xr if v == 0 else []))
-            for t in range(2):
-                mine = X[64 * t:64 * t + 64, 2048 * t:2048 * t + 2048]
-                if last:
-                    dma("Y", T.yx[64 * h:64 * h + 64, 2048 * t:2048 * t + 2048], mine, "out", 16 * (4 + 16 * NJ), [("X", h, t)], (), 3500)
-                else:
-                    dma("Y", X[64 - 64 * t:128 - 64 * t, 2048 * t:2048 * t + 2048], mine, "tw%d" % h, 32 * (v + 1), (), [("X", h, t)], 3500)
+        act(T.ps[:, :, c], pD[:, 0:3, c], F.Sign, 192, dk[0:3], [k("ps")], ["D"], bias=0.5)
         mm = []
-        for i, q in enumerate((0, 2, 3)):
-            mm += group(d[i], [(bc[q], cb), (RT, at)], W)
-        pe(mm, bck + wbk + [k("cb"), k("at")], dk[0:3], ["D"])
-        act(T.sq[:, :, c], d3, F.Square, 3 * W, dk[0:3], [k("sq")], ["D"])
-        sq = [T.sq[:, i, c] for i in range(3)]
-        mm = group(pK[:, 0, c], [(bc[4], cb), (RTH, at), (NIH, sq[0])], W)
-        mm += group(pK[:, 1, c], [(bc[6], cb), (RTH, at), (NIH, sq[1])], W)
-        mm += group(pK[:, 2, c], [(bc[5], cb), (NRT, at), (IH, sq[0]), (IH, sq[1])], W)
-        mm += group(pK[:, 3, c], [(bc[7], cb), (NRTH, at), (IH, sq[2])], W)
-        K = k("K")
-        pe(mm, bck + [k("cb"), k("at"), k("sq"), "RX0", "RX1", "RX2", "ID2", "ID3"], [K], ["K"])
-        tt(T.FM[:, :, c], pK[:, 0:3, c], MS, A.mult, 3 * W, [K, k("MS")], [k("FM")], ["K"])
-        pe([(pO, I1 if STAR else I2, T.FM[:, i, c], STAR and i == 0, i == 2, W) for i in range(3)], [k("FM"), "ID0", "ID1"], ["O"], [OB])
-        ov = pV[:, 2, c]
-        ts(ov, pO, thr, None, A.is_gt, None, W, ["O", ("thr", h)], [k("ov")], [OB, "V"])
-        if not last and j == NJ - 1:
-            a = pD[:, 3, W * j + 16:W * j + 17]
-            pe(group(a, [(T.AW[:], T.acc[:, q:q + 1]) for q in range(NJ)], 256), ["AW"] + [("acc", q) for q in range(NJ)], dk[3:], ["D"])
-            cp(T.ai[:, 0:1], a, 1, dk[3:], ["ai"], ["D"])
-            ts(T.ai[:, 0:1], T.ai[:, 0:1], 31, None, A.bitwise_and, None, 1, ["ai"], ["ai"])
-            tt(thr, T.ai[:, 0:1], T["thi%d" % h][:, 0:1], A.add, 1, ["ai"], [("thr", h)])
-        DD, PR, ab, f02 = T.DD[:, :, c], T.PR[:, :, c], pV[:, 0:2, c], pK[:, 0:2, c]
-        lo, mid, hi = ST[:, 0:2, c], ST[:, 1:3, c], ST[:, 2:4, c]
-        kd, kp, ka, kh = k("DD"), k("PR"), k("ab"), [k("h0"), k("h1")]
-        tt(DD, hi, mid, A.subtract, 4 * W, sk[1:], [kd])
-        tt(ab, f02, DD, A.mult, 2 * W, [K, kd], [ka], ["K", "V"])
-        tt(hi, hi, ab, A.subtract, 2 * W, [ka], sk[2:], ["V"])
-        tt(mid, mid, ab, A.add, 2 * W, [ka], sk[1:3], ["V"])
-        tt(PR, lo, hi, A.mult, 4 * W, sk, [kp])
-        ts(PR, PR, 5, None, A.arith_shift_right, None, 2 * W, (), [kp])
-        ts(PR, PR, CX[:, 4:5], None, A.add, None, 2 * W, ["CX4"], [kp])
         for i in range(2):
-            tt(pV[:, i, c], ov, T.PR[:, i, c], A.mult, W, [k("ov"), kp, ka], [kh[i]], ["V"])
-        tt(hi, hi, ab, A.add, 2 * W, kh, sk[2:] + [ka], ["V"])
-        ts(hi, hi, 4095, None, A.bitwise_and, None, 2 * W, (), sk[2:])
-        tt(DD, hi, lo, A.subtract, 4 * W, sk, [kd])
-        for i in range(2):
-            tt(pV[:, i, c], pK[:, 3, c], T.DD[:, i, c], A.mult, W, [K, kd, ka], [kh[i]], ["K", "V"])
-        R = T["RF%d" % h] if last else ST
-        tt(R[:, 0:2, c], lo, ab, A.add, 2 * W, kh, sk[0:2], ["V"])
+            mm += group(pA[:, i, c], [(wb[7 + i], cb)] + [(wt[4 + q], T.ps[:, q, c]) for q in range(3)])
+        pe(mm, wbk + ["WT1", k("ps"), k("cb")], ak[0:2], ["A"])
+        act(AT[:, :, c], pA[:, 0:2, c], F.Relu, 128, ak[0:2], [k("AT")], ["A"], bias=-16.0)
+        mm = group(pD[:, 0, c], [(wb[11], cb), (wb[9], AT[:, 0, c])]) + group(pD[:, 1, c], [(wb[12], cb), (wb[9], AT[:, 1, c])])
+        for i in (2, 3):
+            mm += group(pD[:, i, c], [(wb[13], cb), (wb[10], AT[:, 0, c])])
+        pe(mm, wbk + [k("cb"), k("AT")], dk, ["D"])
+        act(fm[:, :, c], pD[:, :, c], F.Copy, 256, dk, [("fm", h, j)], ["D"])
+
+    def blend(v, h, xr):
+        X, AT = T["X%d" % h], T.AT
+        last = v == VI - 1
+        twin = TWIN_SCATTER and not last
+        n = 2 if twin else 1
+        at = [("AT", 0), ("AT", 1)]
+        for i in range(n):
+            pe(group(pA[:, 3, 8 * i:8 * i + 8], [(I1, T.CK[:, 8 * i:8 * i + 8])] +
+                     [(T.MI[:, 144 * i + 15 - r:144 * i + 143 - r], AT[:, 0, r:128:16]) for r in range(16)], 64),
+               ["MI0", "MI1", "ID0", "CK0", "CK1"] + at, [("Ax", i)], ["A"])
+        ts(T.ix[:, 0:8], pA[:, 3, 0:8], cx[11], None, A.add, None, 8, ["CX11", ("Ax", 0)], ["ix0"], ["A"])
+        cp(T.ix[:, 8:8 + 8 * n], pA[:, 3, 0:8 * n], 16, [("Ax", 0), ("Ax", 1)], ["ix1"], ["A"])
+        act(T.bg[:], X[:, 0:6144].indirect(T.ix[:, 0:16]), F.Copy, 256 * GCY, xr + [("P", h, 0, q) for q in range(4)] + ["ix0", "ix1"], ["bg"])
+        mm = []
+        for i in range(n):
+            mm += group(pK[:, 2 + i, :], [((I1, SW)[i], T.bg[:, 0:128]), ((I1, SW)[i], T.bg[:, 128:256])], 128)
+        pe(mm, ["bg", "ID0", "ID6"], ["Kb"], ["K"])
+        act(T.br[:, 0:128 * n], pK[:, 2:2 + n, :], F.Identity, 128 * n, ["Kb"], ["br"], ["K"], scale=0.5, bias=127.8)
+        xk = [("X", h, 0), ("X", h, 1)]
+        tt(X[:, 0:4096].indirect(T.ix[:, 8:8 + 8 * n]), T.br[:, 0:128 * n], T.NEG[:, 0:128 * n], A.add, 128 * n * SCAT,
+           ["br", "NEG", "ix1"], xk + (xr if v == 0 else []))
+        for t in range(2):
+            mine = X[64 * t:64 * t + 64, 2048 * t:2048 * t + 2048]
+            if last:
+                dma("Y", T.yx[64 * h:64 * h + 64, 2048 * t:2048 * t + 2048], mine, "out", OUTS, [("X", h, t)], (), 3000)
+            elif not twin:
+                dma("Y", X[64 - 64 * t:128 - 64 * t, 2048 * t:2048 * t + 2048], mine, "tw%d" % h, 32 * (v + 1), (), [("X", h, t)], 3500)
         if not last:
-            cp(U[:, 0, c], R[:, 0, c], W, [sk[0]], [("U", h, j, 0)])
-        mid, rhi = R[:, 1:3, c], R[:, 2:4, c]
-        tt(rhi, hi, ab, A.subtract, 2 * W, kh, sk[2:], ["V"])
-        tt(DD, rhi, mid, A.subtract, 4 * W, sk[1:], [kd])
-        tt(ab, f02, DD, A.mult, 2 * W, [K, kd], [ka] + kh, ["K", "V"])
-        tt(mid, mid, ab, A.add, 2 * W, [ka], sk[1:3], ["V"])
-        tt(rhi, rhi, ab, A.subtract, 2 * W, [ka], sk[2:], ["V"])
-        NX = T["LF%d" % h] if last else T["ST%d%d" % (v + 1, h)]
-        ar = ["ar%d%d%d%d" % (v, h, j, s) for s in range(4)]
+            a = pA[:, 3, 64:65]
+            pe(group(a, [(T.AW[:], T.acc[:, 0:1]), (T.AW[:], T.acc[:, 1:2])], 256), ["AW", ("acc", 0), ("acc", 1)], ["Aa"], ["A"])
+            cp(T.ai[:, h:h + 1], a, 1, ["Aa"], [("ai", h)], ["A"])
+            ts(T.ai[:, h:h + 1], T.ai[:, h:h + 1], 31, None, A.bitwise_and, None, 1, (), [("ai", h)])
+
+    def strands(v, h, j):
+        MS, fm, U = T["MS%d" % h], T["fm%d" % h], T["U%d" % h]
+        SC, R = T["SC%d" % h], T["R%d" % h]
+        c = slice(64 * j, 64 * j + 64)
+        last = v == VI - 1
+        s = [SC[:, v, i, c] for i in range(7)]
+        sk = [("SC", v, h, j, i) for i in range(7)]
+        nx = [SC[:, v + 1, i, c] for i in range(7)]
+        nk = [("SC", v + 1, h, j, i) for i in range(7)]
+        ek, kk = [[(n, j, i) for i in range(4)] for n in "EK"]
+        thr, f, ov, HC, ms = T["thr%d" % h][:, 0:1], ("fm", h, j), T.ov[:, c], T.HC, ("MS", h, j)
+        idk = ["ID0", "ID1"]
+        f02, e01, e23, k01 = fm[:, 0:2, c], pE[:, 0:2, c], pE[:, 2:4, c], pK[:, 0:2, c]
+
+        def k(name):
+            return (name, j)
+        pe(group(pE[:, 0, c], [(I1, s[2]), (NI, s[1])]) + group(pE[:, 1, c], [(I1, s[2]), (NI, s[3])]) +
+           group(pE[:, 2, c], [(PM, MS[:, 0, c]), (NPM, MS[:, 1, c])]) + group(pE[:, 3, c], [(PM, MS[:, 2, c]), (NPM, MS[:, 1, c])]),
+           idk + sk[1:4] + [ms, "PM", "NPM"], ek, ["E"])
+        tt(T.FM[:, :, c], f02, e23, A.mult, 128, [f] + ek[2:], [k("FM")], ["E"])
+        pe(group(pE[:, 2, c], [(PM, MS[:, 1, c]), (I1, T.FM[:, 0, c]), (I1, T.FM[:, 1, c])]), [ms, "PM", "ID0", k("FM")], ek[2:3], ["E"])
+        tt(k01, f02, e01, A.mult, 128, [f] + ek[0:2], kk[0:2], ["E", "K"])
+        tt(SC[:, v, 4:6, c], SC[:, v, 1:4:2, c], k01, A.add, 128, kk[0:2] + [sk[1], sk[3]], sk[4:6], ["K"])
+        ts(ov, pE[:, 2, c], thr, None, A.is_gt, None, 64, ek[2:3] + [("thr", h)], [k("ov")], ["E"])
+        if not last and j == 1:
+            tt(thr, T.ai[:, h:h + 1], T["thi%d" % h][:, 0:1], A.add, 1, [("ai", h)], [("thr", h)])
+        one = T.ONE[:, 0:64]
+        pe(group(pE[:, 0, c], [(I1, s[0]), (I4096, ov)]) + group(pE[:, 1, c], [(I1, s[4]), (I4096, ov)]) +
+           group(pE[:, 2, c], [(I2048, one), (I1, s[1]), (I1, s[2]), (I1, s[3]), (NI, s[4]), (NI, s[5])]) +
+           group(pE[:, 3, c], [(I2048, one), (I1, s[5])]), idk + ["ID3", "ID4", "ONE", k("ov")] + sk[0:6], ek, ["E"])
+        act(T.mm[:, :, c], e01, F.Relu, 128, ek[0:2], [k("mm")], ["E"], bias=-2048.0)
+        pe(group(pK[:, 0, c], [(IOFF, one), (I32, s[1]), (I32, s[2]), (I32, s[3]), (N32, s[4]), (N32, s[5]), (W37, ov)]) +
+           group(pK[:, 1, c], [(IOFF, one), (I32, s[5]), (W37, ov)]), ["ID2", "ID5", "ID7", "W37", "ONE", k("ov")] + sk[1:6], kk[0:2], ["K"])
+        PR, TI = T.PR[:, :, c], T.TI[:, :, c]
+        tt(PR, T.mm[:, :, c], e23, A.mult, 128, [k("mm")] + ek[2:], [k("PR")], ["E"])
+        tt(TI, PR, k01, A.add, 128, [k("PR")] + kk[0:2], [k("TI")], ["K"])
+        ts(TI, TI, 5, 4095, A.arith_shift_right, A.bitwise_and, 128, (), [k("TI")])
+        ts(HC[:, :, c], TI, -2048.0, None, A.add, None, 128, [k("TI")], [k("HC")])
+        pe(group(pE[:, 0, c], [(NI, s[0]), (I1, HC[:, 0, c])]) + group(pE[:, 1, c], [(NI, s[4]), (I1, HC[:, 1, c])]),
+           idk + [k("HC"), sk[0], sk[4]], ek[0:2], ["E"])
+        tt(k01, fm[:, 2:4, c], e01, A.mult, 128, [f] + ek[0:2], kk[0:2], ["E", "K"])
+        tt(SC[:, v + 1, 0:5:4, c], SC[:, v, 0:5:4, c], k01, A.add, 128, kk[0:2] + [sk[0], sk[4]], [nk[0], nk[4]], ["K"])
+        tt(SC[:, v + 1, 5:7, c], HC[:, :, c], k01, A.subtract, 128, kk[0:2] + [k("HC")], nk[5:7], ["K"])
+        pe(group(pE[:, 2, c], [(NI, nx[4]), (I1, nx[5])]) + group(pE[:, 3, c], [(I1, nx[5]), (NI, nx[6])]), idk + nk[4:7], ek[2:], ["E"])
+        tt(k01, f02, e23, A.mult, 128, [f] + ek[2:], kk[0:2], ["E", "K"])
+        rk = [("R", v, h, j, i) for i in range(4)]
+        tt(R[:, v, 1:4:2, c], SC[:, v + 1, 4:7:2, c], k01, A.add, 128, kk[0:2] + [nk[4], nk[6]], [rk[1], rk[3]], ["K"])
+        tt(T.o2[:, 0, c], nx[5], pK[:, 0, c], A.subtract, 64, kk[0:1] + [nk[5]], [k("o2")], ["K"])
+        tt(R[:, v, 2, c], T.o2[:, 0, c], pK[:, 1, c], A.subtract, 64, kk[1:2] + [k("o2")], [rk[2]], ["K"])
+        if not last:
+            ts(U[:, 0, c], nx[0], 2048.0, None, A.add, None, 32, [nk[0]], [("U", h, j, 0)])
+        if JOIN and j == 0:
+            return
+        js = (0, 1) if JOIN else (j,)
+        c = slice(64 * js[0], 64 * js[-1] + 64)
+        arr = ["ar%d%d%d%d" % (v, h, j, i) for i in range(4)]
         trs = []
-        for s in (1, 2, 3):
-            rid, pid, _ = topo.addr(others[s])
-            trs.append(RemoteDMATransfer(dst_ids=[DstId(rid=rid, pnc=pid)], dma_engine_mask=bits(masks[s]), remote_sem=sem[ar[s]],
-                                         src=R[:, s, c], dst=NX[:, s, c]))
-        op("G", 1000, lambda e: g.remote_dma_fused(trs, local_sem=sem.sent), sk[1:], [("mv", v, h, j)], sig=(None, 0))
-        op("E", 0, None, [("mv", v, h, j)], (), sig=("sent", sent * 2 * VI * NJ))
-        nk = [("ST", v + 1, h, j, s) for s in range(4)]
-        for s in (1, 2, 3):
-            op("E", 0, None, [("mv", v, h, j)], [nk[s]], lat=SEND_NS - 1500 * (s in near), sig=(ar[s], len(masks[s])))
+        for i in (1, 2, 3):
+            rid, pid, _ = topo.addr(others[i])
+            trs.append(RemoteDMATransfer(dst_ids=[DstId(rid=rid, pnc=pid)], dma_engine_mask=bits(masks[i]), remote_sem=sem[arr[i]],
+                                         src=R[:, v, i, c], dst=SC[:, v + 1, i, c]))
+        op("G", 900, lambda o: g.remote_dma_fused(trs, local_sem=sem.sent), [("R", v, h, q, i) for q in js for i in (1, 2, 3)],
+           [("mv", v, h, j)], sig=(None, 0))
+        op("D", SEND_BUSY, None, [("mv", v, h, j)], [("mw", v, h, j)], sig=("sent", sent * (2 if JOIN else 4) * VI))
+        for i in (1, 2, 3):
+            op("E", 0, None, [("mw", v, h, j)], [("SC", v + 1, h, q, i) for q in js], lat=SEND_NS - 1000 * (i in near), sig=(arr[i], len(masks[i])))
+        n = 64 * len(js)
         if not last:
-            dma("Y", NX[:, 0, c], R[:, 0, c], ar[0], 16, sk[0:1], nk[0:1], 2200)
-            if ONECONV:
-                cp(U[:, 1:4, c], NX[:, 1:4, c], 3 * W, nk[1:], [("U", h, j, s) for s in (1, 2, 3)])
-            else:
-                for s in (2, 1, 3):
-                    cp(U[:, s, c], NX[:, s, c], W, [nk[s]], [("U", h, j, s)])
-        else:
-            for s in range(4):
-                for t in range(2):
-                    c0 = 256 * s + 128 * t + W * j
-                    dma("S" if (h and t) else "Y", T.ys[64 * h:64 * h + 64, c0:c0 + W], (NX if s else R)[64 * t:64 * t + 64, s, c],
-                        "out", 16 * (4 + 16 * NJ), [nk[s] if s else sk[0]], (), 2200)
+            ts(U[:, 1:4, c], SC[:, v + 1, 1:4, c], 2048.0, None, A.add, None, 1.5 * n,
+               [("SC", v + 1, h, q, i) for q in js for i in (1, 2, 3)], [("U", h, q, i) for q in js for i in (1, 2, 3)])
+            return
+        OF = T["OF%d" % h]
+        for i in (0, 2, 1, 3):
+            ts(OF[:, i, c], SC[:, v + 1, i, c], 2048.0, None, A.add, None, n, [("SC", v + 1, h, q, i) for q in js], [("OF", h, j, i)])
+            for t in range(2):
+                c0 = 256 * i + 128 * t + 64 * js[0]
+                dma("S" if (h and t) else "Y", T.ys[64 * h:64 * h + 64, c0:c0 + n], OF[64 * t:64 * t + 64, i, c],
+                    "out", OUTS, [("OF", h, j, i)], (), 2200)
 
     for v in range(VI):
         for h in range(2):
-            cur[0], cur[1] = 2 * v + h, 0
+            cur[0] = 2 * v + h
             xr = [("X" if v else "Xl", h, t) for t in range(2)]
             if v == 0:
-                cp(T["U%d" % h][:], T["ST0%d" % h][:], 512, [("STl", h, s, t) for s in range(4) for t in range(2)],
-                   [("U", h, j, s) for s in range(4) for j in range(NJ)] + [("ST", 0, h, j, s) for s in range(4) for j in range(NJ)])
-            cur[1] = 0
+                for s in (0, 2, 1, 3):
+                    hk = [("HI", h, s, t) for t in range(2)]
+                    cp(T["U%d" % h][:, s, :], T["HI%d" % h][:, s, :], 128, hk, [("U", h, j, s) for j in range(2)])
+                hk = [("HI", h, s, t) for t in range(2) for s in range(4)]
+                ts(T["SC%d" % h][:, 0, 0:4, :], T["HI%d" % h][:], -2048.0, None, A.add, None, 512, hk,
+                   [("SC", 0, h, j, s) for j in range(2) for s in range(4)])
             for j in range(2):
-                pairs_of_piece(v, h, j, xr)
-            for j in range(NJ):
-                cur[1] = 100 * (j + 1)
-                chunk(v, h, j, xr)
+                costs(v, h, j, xr)
+            for j in range(2):
+                decide(v, h, j)
+            blend(v, h, xr)
+            for j in range(2):
+                strands(v, h, j)
     return ops
-
-
-ONECONV = False
 
 
 def schedule(ops):
@@ -465,25 +534,31 @@ def schedule(ops):
         for i, p in enumerate(pred):
             for d in p:
                 succ[d].append(i)
-        for look, lead in TRIES:
-            prio = [0.0] * len(ops)
-            for o in reversed(ops):
-                prio[o["i"]] = o["dur"] + o["lat"] + 120 + max([prio[s] for s in succ[o["i"]]] + [0.0])
-            prio = [p + lead * (o["h"] == 0) for p, o in zip(prio, ops)]
-            for _ in range(8):
+        tail = [0.0] * len(ops)
+        for o in reversed(ops):
+            tail[o["i"]] = o["dur"] + o["lat"] + 120 + max([tail[s] for s in succ[o["i"]]] + [0.0])
+        for look, lead, bonus in TRIES:
+            prio = [tail[o["i"]] + lead * (o["h"] == 0) - bonus * o["long"] for o in ops]
+            for n in range(ROUNDS):
                 order, start, fin = place(ops, pred, succ, prio, look, False)
                 if max(fin) < PLAN.get("end", 1e18):
-                    PLAN.update({"order": order, "end": max(fin), "start": start})
-                prio = place(ops, succ, pred, fin, look, True)[2]
-    bank = {}
+                    PLAN.update({"order": order, "end": max(fin), "start": start, "by": (look, lead, bonus, n)})
+                if n + 1 < ROUNDS:
+                    prio = place(ops, succ, pred, fin, look, True)[2]
+                    prio = [p - bonus * o["long"] for p, o in zip(prio, ops)]
+    bank, lastacc = {}, {}
     for i in PLAN["order"]:
         o = ops[i]
         o["t"] = PLAN["start"][i]
+        if o["tag"] is not None and o["tag"][0] == "acc":
+            lastacc[o["tag"]] = i
         for b in o["banks"]:
             for e2, d in bank.get(b, {}).items():
                 if e2 != o["eng"]:
                     o["deps"].add(d)
             bank.setdefault(b, {})[o["eng"]] = i
+    for i in lastacc.values():
+        ops[i]["stop"] = True
     return PLAN["order"], PLAN["end"]
 
 
@@ -509,7 +584,7 @@ def place(ops, pred, succ, prio, look, back):
                 for b in ops[i]["banks"]:
                     for e2, d in bank.get(b, {}).items():
                         if e2 != e:
-                            t = max(t, fin[d] + 130)
+                            t = max(t, fin[d] + CROSS)
                 c.append((t, i))
             t0 = min(c)[0]
             if best is None or t0 < best[0]:
@@ -527,7 +602,7 @@ def place(ops, pred, succ, prio, look, back):
         avail[e].remove(i)
         for s in succ[i]:
             e2 = ops[s]["eng"]
-            gap = 0 if (e if back else e2) in "DE" else 70 if e2 == e else 130
+            gap = 0 if (e if back else e2) in "DE" else SAME if e2 == e else CROSS
             base[s] = max(base[s], fin[i] + gap + (ops[s]["lat"] if back else 0))
             left[s] -= 1
             if left[s] == 0:
@@ -549,9 +624,9 @@ def rank_program(g, core, T, topo):
         ne, total = len(topo.engines(core, owner)), 0
         for i in order:
             tag = ops[i]["tag"]
-            if tag is None or hs[tag[2] % len(hs)] != core:
+            if tag is None or tag[0] != "fold" or hs[tag[3] % len(hs)] != core:
                 continue
-            v, h, f = tag
+            v, h, f = tag[1:]
             c0 = 2048 * PAIRS.index(FOLD[f][0:2]) + FOLD[f][2]
             g.wait_ge(T.sem["ha%d%d" % (f, h)], (v + 1) * len(topo.engines(owner, core)))
             g.remote_dma(T["M%d" % h][:, c0:c0 + FOLD[f][3]], helper_slot(T, v, h, f), T.sem["hb%d%d" % (f, h)],
@@ -592,7 +667,7 @@ def rank_program(g, core, T, topo):
             if want[s] > waited.get((e, s), 0):
                 queue[e].wait_ge(T.sem[s], want[s])
                 waited[(e, s)] = want[s]
-        ins = o["fn"](e)
+        ins = o["fn"](o)
         if mark:
             ins.then_inc(T.sem["c" + e], 1)
     for s in sorted(totals):

from concourse.bass import DstId, RemoteDMATransfer
from concourse.mybir import AluOpType, ActivationFunctionType

A = AluOpType
F = ActivationFunctionType
VI = 5
PAIRS = [(0, 1), (2, 3), (0, 2), (1, 3), (0, 3), (1, 2)]
FOLD = [(a, b, c, 1024) for c in (0, 1024) for a, b in ((0, 2), (0, 1), (1, 2))]
SP = 512
MP = 512
VGATHER = []
VFIRST = [(2, 0), (2, 1), (2, 2), (2, 3)]
TWIN_SCATTER = True
JOIN = False
OUTS = 16 * (4 + (16 if JOIN else 32))
CY, GCY, SCAT, PECY, FIX, PFIX = 1.04, 1.56, 3.8, 0.52, 60, 5
SAME, CROSS = 70, 130
FOLD_NS, BACK_NS, SEND_NS, SEND_BUSY = 1850, 2800, 2500, 1300
TRIES = [(a, b, c) for a in (20, 40, 80, 150) for b in (4000, 8000, 12000) for c in (3000, 6000, 10000, 15000)]
ROUNDS = 4

SCRATCH = {}
for _h in range(2):
    SCRATCH["X%d" % _h] = ("sbuf", [128, 4096 + 2048], "bfloat16")
    SCRATCH["P%d" % _h] = ("sbuf", [128, 3 * 2048], "bfloat16")
    SCRATCH["M%d" % _h] = ("sbuf", [128, 6 * 2048], "bfloat16")
    SCRATCH["HI%d" % _h] = ("sbuf", [128, 4, 128], "int32")
    SCRATCH["SC%d" % _h] = ("sbuf", [128, VI + 1, 7, 128], "float16")
    SCRATCH["R%d" % _h] = ("sbuf", [128, VI, 4, 128], "float16")
    SCRATCH["OF%d" % _h] = ("sbuf", [128, 4, 128], "float32")
    SCRATCH["U%d" % _h] = ("sbuf", [128, 4, 128], "uint16")
    SCRATCH["thi%d" % _h] = ("sbuf", [128, 4], "int32")
    SCRATCH["thr%d" % _h] = ("sbuf", [128, 4], "float32")
    SCRATCH["MS%d" % _h] = ("sbuf", [128, 3, 128], "float16")
    SCRATCH["fm%d" % _h] = ("sbuf", [128, 4, 128], "bfloat16")
    SCRATCH["pT%d" % _h] = ("psum", [128, 512], "float32")
for _n, _w, _d in [
    ("sg", 128, "bfloat16"), ("cb", 128, "bfloat16"), ("acc", 4, "float32"), ("ai", 4, "int32"), ("ix", 24, "uint16"),
    ("bg", 256, "bfloat16"), ("br", 256, "bfloat16"), ("ov", 128, "float16"),
    ("CI", 12, "int32"), ("CF", 12, "float32"), ("CX", 20, "float32"), ("J", 144, "float32"), ("JB", 128, "float32"),
    ("JG", 128, "float32"), ("MI", 288, "bfloat16"), ("ID", 11 * 128, "bfloat16"), ("W37", 128, "float16"), ("WP", 512, "bfloat16"),
    ("bm", 8, "bfloat16"), ("AW", 128, "float32"), ("eq", 8, "float32"), ("lam", 8, "float32"), ("WT", 7 * 128, "bfloat16"),
    ("CK", 16, "float16"), ("CJ", 16, "float32"), ("NEG", 256, "bfloat16"), ("ONE", 128, "bfloat16"), ("ZE", 128, "bfloat16"),
    ("RW", 64, "float32"), ("WS", 96, "bfloat16"),
]:
    SCRATCH[_n] = ("sbuf", [128, _w], _d)
for _n, _w, _d in [("LM", 3, "float16"), ("FM", 2, "float16"), ("ps", 3, "bfloat16"), ("AT", 2, "bfloat16"),
                   ("mm", 2, "float32"), ("PR", 2, "float32"), ("TI", 2, "int32"), ("HC", 2, "float16"), ("o2", 1, "float32"),
                   ("WB", 21, "bfloat16")]:
    SCRATCH[_n] = ("sbuf", [128, _w, 128], _d)
SCRATCH["CT"] = ("sbuf", [128, 2, 192], "float16")
SCRATCH["SR"] = ("sbuf", [128, 3, 3], "float32")
SCRATCH["AE"] = ("sbuf", [128, 3, 3, 12], "float32")
SCRATCH["LH"] = ("sbuf", [128, 2, 3, 12], "float32")
SCRATCH["LQ"] = ("sbuf", [128, 4, 3, 12], "float32")
SCRATCH["AR"] = ("sbuf", [128, 21, 16], "bfloat16")
SCRATCH["pC"] = ("psum", [128, 1024], "float32")
for _n in ("pA", "pD", "pE", "pK"):
    SCRATCH[_n] = ("psum", [128, 4, 128], "float32")

SEMAPHORES = ["cV", "cS", "cP", "cG", "thl", "sent", "out", "hsent"]
for _h in range(2):
    SEMAPHORES += ["xl%d" % _h, "tw%d" % _h, "lf%d0" % _h, "lf%d1" % _h] + ["hl%d%d" % (_h, _s) for _s in range(4)]
    SEMAPHORES += ["ar%d%d%d%d" % (_v, _h, _j, _s) for _v in range(VI) for _j in range(2) for _s in range(1, 4)]
    SEMAPHORES += ["ha%d%d" % (_f, _h) for _f in range(len(FOLD))] + ["hb%d%d" % (_f, _h) for _f in range(len(FOLD))]


def helpers_of(core, T, topo):
    return [c for c in topo.cores_of(core) if T.rank_of(c) is None and topo.die(c) == topo.die(core)]


def bits(engines):
    m = 0
    for e in engines:
        m |= 1 << e
    return m


def helper_slot(T, v, h, f):
    n = (2 * v + h) * ((len(FOLD) + 2) // 3) + f // 3
    name, j = [("M0", n), ("M1", n - 12), ("P0", n - 24), ("P1", n - 30)][0 if n < 12 else 1 if n < 24 else 2 if n < 30 else 3]
    return T[name][:, j * 1024:j * 1024 + FOLD[f][3]]


def build(g, core, T, topo):
    ops, lastw, readers, cur = [], {}, {}, [0]
    rank = T.rank_of(core)
    sem = T.sem

    def op(eng, dur, fn, r=(), w=(), banks=(), lat=0, sig=None, tag=None):
        o = {"eng": eng, "dur": dur, "fn": fn, "banks": banks, "lat": lat, "sig": sig, "deps": set(), "i": len(ops), "tag": tag,
             "h": cur[0] % 2, "u": cur[0], "stop": False, "w": list(w)[0:2], "long": False}
        for k in r:
            if k in lastw:
                o["deps"].update(lastw[k])
        for k in w:
            o["deps"].update(lastw.get(k, ()))
            o["deps"].update(readers.get(k, ()))
        for k in r:
            readers.setdefault(k, []).append(o["i"])
        for k in w:
            lastw[k] = [o["i"]]
            readers[k] = []
        o["deps"].discard(o["i"])
        ops.append(o)
        return o

    def vec(n, fn, r, w, banks=()):
        return op("V", FIX + max(64, n) * CY, lambda o: fn(g.vector), r, w, banks)

    def ts(out, in0, s1, s2, o0, o1, n, r, w, banks=()):
        if o1 is None:
            return vec(n, lambda q: q.tensor_scalar(out, in0, s1, None, o0), r, w, banks)
        return vec(n, lambda q: q.tensor_scalar(out, in0, s1, s2, o0, o1), r, w, banks)

    def tt(out, in0, in1, o, n, r, w, banks=()):
        return vec(n, lambda q: q.tensor_tensor(out, in0, in1, o), r, w, banks)

    def cp(out, in_, n, r, w, banks=()):
        return vec(n, lambda q: q.tensor_copy(out, in_), r, w, banks)

    def act(out, in_, func, n, r, w, banks=(), **kw):
        return op("S", FIX + 20 + max(64, n) * CY, lambda o: g.scalar.activation(out, in_, func, **kw), r, w, banks)

    def pe(mms, r, w, banks, tag=None):
        def fn(o):
            last = None
            for i, m in enumerate(mms):
                stop = m[4] if m[4] is not None else (o["stop"] and i == len(mms) - 1)
                last = g.tensor.matmul(m[0], m[1], m[2], m[3], stop)
            return last
        return op("P", sum([max(64, m[5]) * PECY + PFIX for m in mms]), fn, r, w, banks, lat=60, tag=tag)

    def group(out, terms, n=64):
        return [(out, a, b, i == 0, i == len(terms) - 1, n) for i, (a, b) in enumerate(terms)]

    def dma(eng, out, in_, s, total, r, w, lat):
        q = g.sync if eng == "Y" else g.scalar
        return op(eng, 100, lambda o: q.dma_start(out, in_).then_inc(sem[s], 16), r, w, lat=lat, sig=(s, total))

    def iota(out, pattern, base, cm, w, n, flag=True):
        if flag:
            return op("G", 160 + 2 * n * CY, lambda o: g.iota(out, pattern, base, cm, allow_small_or_imprecise_dtypes=True), (), w)
        return op("G", 160 + 2 * n * CY, lambda o: g.iota(out, pattern, base, cm), (), w)

    for h in range(2):
        cur[0] = h
        for s in (0, 2, 1, 3):
            for t in range(2):
                dma("Y" if (h or t) else "S", T["HI%d" % h][64 * t:64 * t + 64, s, :],
                    T.hom[64 * h:64 * h + 64, 256 * s + 128 * t:256 * s + 128 * t + 128], "hl%d%d" % (h, s), 32, (), [("HI", h, s, t)], 2200)
            if s == 0:
                for t in range(2):
                    dma("Y" if (h or t) else "S", T["X%d" % h][64 * t:64 * t + 64, 0:4096], T.x[64 * h:64 * h + 64, :], "xl%d" % h, 32, (),
                        [("Xl", h, t)], 4000 + 3500 * h)
    cur[0] = 0
    CI, CF, CX, J, ID, AR, WB, RW = T.CI, T.CF, T.CX, T.J, T.ID, T.AR, T.WB, T.RW
    iota(CI[:, 0:1], [[0, 1]], 0, 1, ["CI0"], 1, False)
    iota(J[:], [[1, 144]], 0, 0, ["J"], 144)
    iota(T.JB[:], [[16, 8], [0, 16]], 0, 0, ["JB"], 128)
    iota(T.AE[:, 0], [[0, 4], [1, 9]], 4, 0, ["AE0"], 36)
    iota(T.AE[:, 1], [[1, 4], [1, 9]], 5, 0, ["AE1"], 36)
    iota(RW[:, 0:16], [[0, 2], [1, 8]], 0, 0, ["RW0"], 16)
    iota(RW[:, 16:32], [[1, 2], [0, 8]], 0, 0, ["RW1"], 16)
    iota(T.CJ[:], [[0, 2], [256, 8]], 4, 0, ["CJ"], 16)
    iota(T.JG[:], [[0, 2], [1, 4], [0, 16]], 0, 0, ["JG"], 128)
    for h in range(2):
        for t in range(2):
            op("G", 600, lambda o, h=h, t=t: g.dma_start(T["thi%d" % h][64 * t:64 * t + 64, 0:1], T.th[64 * h:64 * h + 64, :],
                                                          allow_slow_non_contiguous=True).then_inc(sem.thl, 16),
               (), [("thl", h, t)], lat=3000, sig=("thl", 64))
    q0 = CI[:, 0:1]
    ts(CI[:, 1:2], q0, 15, None, A.bitwise_and, None, 1, ["CI0"], ["CI1"])
    ts(CI[:, 2:3], q0, 2, 3, A.arith_shift_right, A.bitwise_and, 1, ["CI0"], ["CI2"])
    ts(CI[:, 3:4], q0, 3, None, A.bitwise_and, None, 1, ["CI0"], ["CI3"])
    ts(CI[:, 4:5], q0, 112, None, A.bitwise_and, None, 1, ["CI0"], ["CI4"])
    ts(CI[:, 5:6], q0, 4, 3, A.arith_shift_right, A.bitwise_and, 1, ["CI0"], ["CI5"])
    ts(CI[:, 6:7], q0, 64, None, A.bitwise_and, None, 1, ["CI0"], ["CI6"])
    ts(CI[:, 7:8], q0, 3, 1, A.arith_shift_right, A.bitwise_and, 1, ["CI0"], ["CI7"])
    ts(CI[:, 8:9], q0, 7, None, A.bitwise_and, None, 1, ["CI0"], ["CI8"])
    cp(CF[:, 0:9], CI[:, 0:9], 9, ["CI%d" % i for i in range(9)], ["CF"])
    qf, kf, Lf, Rf, bf, gf, tf, xf, jf = [CF[:, i:i + 1] for i in range(9)]
    ts(T.bm[:], T.JB[:, 0:128:16], bf, None, A.is_equal, None, 8, ["JB", "CF"], ["bm"])
    vec(64, lambda q: q.memset(T.ZE[:], 0.0), (), ["ZE"])
    vec(64, lambda q: q.memset(T.WS[:], 0.0), (), ["WS"])
    for p in range(3):
        ts(T.WS[:, 32 * p:32 * p + 8], T.bm[:], 2.0, None, A.mult, None, 8, ["bm", "WS"], ["WS%d" % p])
        ts(T.WS[:, 72 + 8 * p:80 + 8 * p], T.bm[:], -1.0, None, A.mult, None, 8, ["bm", "WS"], ["WN%d" % p])
    wsum = [T.WS[:, 24 * p:24 * p + 24] for p in range(4)]
    wsk = [["WS0"], ["WS1"], ["WS2"], ["WN0", "WN1", "WN2"]]
    cols = [(kf, 4.0, None, A.is_lt, None), (kf, 12.0, None, A.is_ge, None), (xf, 1024.0, -1024.0, A.mult, A.add), (xf, -1024.0, None, A.mult, None),
            (jf, 4.0, None, A.add, None), (jf, 5.0, None, A.add, None), (xf, -2.0, 1.0, A.mult, A.add), (xf, 2.0, -1.0, A.mult, A.add),
            (xf, -1.0, None, A.add, None), (kf, -4.0, None, A.add, None), (kf, 1184.0, None, A.mult, None), (tf, -32.0, 4096.0, A.mult, A.add),
            (tf, -2.0, 64.0, A.mult, A.add), (kf, 16.0, None, A.mult, None)]
    for i, c in enumerate(cols):
        ts(CX[:, i:i + 1], c[0], c[1], c[2], c[3], c[4], 1, ["CF"], ["CX%d" % i])
    cx = [CX[:, i:i + 1] for i in range(20)]
    ts(cx[14], cx[12], qf, None, A.add, None, 1, ["CX12", "CF"], ["CX14"])
    ts(cx[12], cx[12], bf, None, A.add, None, 1, ["CX14", "CF"], ["CX12"])
    ts(cx[15], jf, 1.0, cx[8], A.add, A.mult, 1, ["CF", "CX8"], ["CX15"])
    I1, NI, I32, I4096, I2048, IOFF, SW, N32, PMT, PM, NPM = [ID[:, 128 * i:128 * i + 128] for i in range(11)]
    ts(I1, J[:, 0:128], qf, None, A.is_equal, None, 128, ["J", "CF"], ["ID0"])
    for i, c in ((1, -1.0), (2, 32.0), (3, 4096.0), (4, 2048.0), (5, -127.0 * 65536), (7, -32.0)):
        act(ID[:, 128 * i:128 * i + 128], I1, F.Copy, 128, ["ID0"], ["ID%d" % i], scale=c)
    ts(SW, J[:, 0:128], cx[14], None, A.is_equal, None, 128, ["J", "CX14"], ["ID6"])
    W37 = T.W37[:]
    ts(W37, I1, cx[10], None, A.mult, None, 128, ["ID0", "CX10"], ["W37"])
    ts(cx[16], xf, 64.0, jf, A.mult, A.add, 1, ["CF"], ["CX16"])
    ts(cx[17], bf, 0.5, cx[16], A.mult, A.add, 1, ["CF", "CX16"], ["CX17"])
    ts(PMT, J[:, 0:128], cx[17], None, A.is_equal, None, 128, ["J", "CX17"], ["PMT"])
    for i, c in enumerate((bf, cx[12])):
        ts(T.MI[:, 144 * i:144 * i + 144], J[:], 15.0, c, A.subtract, A.is_equal, 144, ["J", "CF", "CX12"], ["MI%d" % i])
        ts(T.MI[:, 144 * i:144 * i + 144], T.MI[:, 144 * i:144 * i + 144], cx[15], -1.0, A.mult, A.mult, 72, ["CX15"], ["MI%d" % i])
    ts(T.CJ[:], T.CJ[:], cx[13], None, A.add, None, 16, ["CX13"], ["CJ"])
    ts(T.CK[:, 0:8], T.CJ[:, 0:8], cx[11], 4096.0, A.subtract, A.add, 8, ["CJ", "CX11"], ["CK0"])
    ts(T.CK[:, 8:16], T.CJ[:, 8:16], cx[11], -2048.0, A.add, A.add, 8, ["CJ", "CX11"], ["CK1"])
    eq, lam = T.eq, T.lam
    ts(eq[:, 0:3], J[:, 0:3], Lf, None, A.is_equal, None, 3, ["J", "CF"], ["eqL"])
    ts(eq[:, 4:7], J[:, 0:3], Rf, None, A.is_equal, None, 3, ["J", "CF"], ["eqR"])
    tt(lam[:, 0:3], eq[:, 0:3], eq[:, 4:7], A.subtract, 3, ["eqL", "eqR"], ["lam"])
    tt(lam[:, 4:7], eq[:, 4:7], eq[:, 0:3], A.subtract, 3, ["eqL", "eqR"], ["nlam"])
    tt(lam[:, 3:4], Lf, Rf, A.not_equal, 1, ["CF"], ["sw"])
    sw = lam[:, 3:4]
    ts(T.AW[:], T.JG[:], gf, sw, A.is_equal, A.mult, 128, ["JG", "CF", "sw"], ["AW"])
    vec(88, lambda q: q.memset(AR[:], 0.0), (), ["AR"])
    vec(128, lambda q: q.memset(T.NEG[:], -128.0), (), ["NEG"])
    vec(64, lambda q: q.memset(T.ONE[:], 1.0), (), ["ONE"])
    SR = T.SR
    vec(9, lambda q: q.memset(SR[:], 0.0), (), ["SR"])
    for i, (a, c) in enumerate(((SR[:, 0, 0:2], -1.0), (SR[:, 1, 2:3], -1.0), (SR[:, 1, 0:1], 1.0), (SR[:, 2, 1:3], 1.0))):
        vec(2, lambda q, a=a, c=c: q.memset(a, c), ["SR"], ["SR%d" % i])
    srk = ["SR0", "SR1", "SR2", "SR3", "AR"]
    ark = []

    def ar(fn, out, *args):
        ark.append("AR%d" % len(ark))
        fn(out, *(args[:-1] + (args[-1] + ["AR"], [ark[-1]])))
    ar(ts, AR[:, 0:3, 0:3], SR[:], cx[0], None, A.mult, None, 9, srk + ["CX0"])
    ar(ts, AR[:, 0:3, 3:6], SR[:], cx[1], None, A.mult, None, 9, srk + ["CX1"])
    ar(ts, AR[:, 15:18, 0:3], SR[:], cx[2], None, A.mult, None, 9, srk + ["CX2"])
    ar(ts, AR[:, 15:18, 3:6], SR[:], cx[3], None, A.mult, None, 9, srk + ["CX3"])
    AE, LH, LQ = T.AE, T.LH, T.LQ
    ts(AE[:, 2], AE[:, 1], 13.0, -9.0, A.is_ge, A.mult, 36, ["AE1"], ["AE2"])
    tt(AE[:, 2], AE[:, 2], AE[:, 1], A.add, 72, ["AE1", "AE2"], ["AE2"])
    tt(LH[:, 0], AE[:, 0], AE[:, 2], A.min, 72, ["AE0", "AE2"], ["LH0"])
    tt(LH[:, 1], AE[:, 0], AE[:, 2], A.max, 72, ["AE0", "AE2"], ["LH1"])
    for i in range(2):
        ts(LQ[:, i], LH[:, i], cx[4], cx[6], A.is_le, A.mult, 36, ["LH%d" % i, "CX4", "CX6"], ["LQ%d" % i])
        ts(LQ[:, 2 + i], LH[:, i], cx[5], 2.0, A.is_equal, A.mult, 36, ["LH%d" % i, "CX5"], ["LQ%d" % (2 + i)])
    ar(tt, AR[:, 3:6, 0:12], LQ[:, 0], LQ[:, 1], A.subtract, 72, ["LQ0", "LQ1"])
    ar(tt, AR[:, 18:21, 0:12], LQ[:, 2], LQ[:, 3], A.subtract, 72, ["LQ2", "LQ3"])
    for i in range(2):
        c = 4 * i
        ar(ts, AR[:, 14, 3 * i:3 * i + 2], eq[:, c + 1:c + 3], eq[:, c:c + 1], -1.0, A.subtract, A.mult, 2, ["eqL", "eqR"])
        ar(tt, AR[:, 14, 3 * i + 2:3 * i + 3], eq[:, c + 1:c + 2], eq[:, c + 2:c + 3], A.subtract, 2, ["eqL", "eqR"])
    ar(ts, AR[:, 6, :], RW[:, 0:16], cx[9], None, A.is_equal, None, 16, ["RW0", "CX9"])
    ts(RW[:, 32:48], J[:, 0:16], 4.0, None, A.is_ge, None, 16, ["J"], ["RW2"])
    for i in range(2):
        ar(ts, AR[:, 7 + i, :], RW[:, 16:32], lam[:, 2 * i:2 * i + 1], sw, A.mult, A.add, 16, ["RW1", "lam", "sw"])
        ar(ts, AR[:, 9 + i, 4:16], J[:, 4:16], cx[5], cx[7 + i], A.is_lt, A.mult, 16, ["J", "CX5", "CX7", "CX8"])
        ar(ts, AR[:, 11 + i, :], RW[:, 32:48], lam[:, 4 + 2 * i:5 + 2 * i], eq[:, 2 * i:2 * i + 1], A.mult, A.add, 16, ["RW2", "nlam", "eqL"])
    ar(ts, AR[:, 13, :], RW[:, 32:48], sw, None, A.mult, None, 16, ["RW2", "sw"])
    for b in range(8):
        ts(WB[:, :, 16 * b:16 * b + 16], AR[:], T.bm[:, b:b + 1], None, A.mult, None, 168, ark + ["bm"], ["WB%d" % b])
    wbk = ["WB%d" % b for b in range(8)]
    pA, pD, pE, pK, pC = T.pA, T.pD, T.pE, T.pK, T.pC
    ak, dk, ek = [[(n, j, i) for j in range(2) for i in range(4)] for n in "ADE"]
    pe([(pE[:, i, :], PMT, WB[:, w, :], True, True, 128) for i, w in enumerate((0, 1, 2, 6))], wbk + ["PMT"], ek, ["E"])
    act(T.WP[:], pE[:], F.Copy, 512, ek, ["WP"], ["E"])
    wp = [T.WP[:, 128 * i:128 * i + 128] for i in range(4)]
    pe([(pK[:, 0, :], PMT, I1, True, True, 128)], ["PMT", "ID0"], [("K", 0, 0), ("K", 1, 0)], ["K"])
    act(PM, pK[:, 0, :], F.Copy, 128, [("K", 0, 0), ("K", 1, 0)], ["PM"], ["K"])
    act(NPM, pK[:, 0, :], F.Copy, 128, [("K", 0, 0), ("K", 1, 0)], ["NPM"], ["K"], scale=-1.0)
    pe([(pD[:, j, :], WB[:, 14 + j, :], I1, True, True, 128) for j in range(4)], wbk + ["ID0"], dk, ["D"])
    pe([(pA[:, j, :], WB[:, 18 + j, :], I1, True, True, 128) for j in range(3)], wbk + ["ID0"], ak + [("Ax", 0), ("Ax", 1), "Aa"], ["A"])
    act(T.WT[:, 0:512], pD[:], F.Copy, 512, dk, ["WT0"], ["D"])
    act(T.WT[:, 512:896], pA[:, 0:3, :], F.Copy, 384, ak, ["WT1"], ["A"])
    wt = [T.WT[:, 128 * i:128 * i + 128] for i in range(7)]
    wb = [WB[:, i, :] for i in range(14)]
    for h in range(2):
        cp(T["thr%d" % h][:, 0:1], T["thi%d" % h][:, 0:1], 1, [("thl", a, b) for a in range(2) for b in range(2)], [("thr", h)])

    others = [T.cores[(rank + s) % len(T.cores)] for s in range(4)]
    helpers = helpers_of(core, T, topo)
    far = [s for s in (1, 2, 3) if topo.chip(others[s]) != topo.chip(core)]
    masks, used = {}, []
    for i, s in enumerate(far):
        e = topo.engines(core, others[s])
        masks[s] = e[i * len(e) // len(far):(i + 1) * len(e) // len(far)]
        used += masks[s]
    near = [s for s in (1, 2, 3) if s not in far]
    for i, s in enumerate(near):
        e = [x for x in topo.engines(core, others[s]) if x not in used]
        masks[s] = e[i * len(e) // len(near):(i + 1) * len(e) // len(near)]
    sent = sum([len(masks[s]) for s in (1, 2, 3)])
    crot = [0]

    def costs(v, h, j, xr):
        X, P, M, U, pT = T["X%d" % h], T["P%d" % h], T["M%d" % h], T["U%d" % h], T["pT%d" % j]
        bank, lo, mine = ["T%d" % j], 1024 * j, (2 * j, 2 * j + 1)
        first = len(ops)

        def ps(s, a, b, step=1):
            return X[:, 4096 + a:4096 + b:step] if s == 0 else P[:, 2048 * (s - 1) + a:2048 * (s - 1) + b:step]

        def add_sums(tile, w, r, name):
            pe([(pT[:, k:192:8], tile(k), wsum[w], False, None, 64) for k in range(8)], r + wsk[w] + [("Tz", j)], [("Ts", j, name)], bank,
               tag=("acc", v, h, j))
        pe([(pT[:, 0:192], T.ZE[:], ID[:, 0:192], True, False, 192)], ["ZE", "ID0", "ID1"], [("Tz", j)], bank)
        onv = VFIRST if (v, h) == (0, 0) else VGATHER
        for s in (0, 2, 1, 3):
            whole = SP == 1024 and not [q for q in mine if (s, q) in onv]
            for q, n in ([(mine[0], 2)] if whole else [(q, 1) for q in mine]):
                win = X[:, 0:4096].indirect(U[:, s, 32 * q:32 * (q + n)])
                rk, wk = xr + [("U", h, j, s)], [("P", h, s, q + i) for i in range(n)]
                if (s, q) in onv:
                    cp(ps(s, 512 * q, 512 * (q + n)), win, 512 * n * GCY, rk, wk)
                else:
                    act(ps(s, 512 * q, 512 * (q + n)), win, F.Copy, 512 * n * GCY, rk, wk)
            add_sums(lambda k, s=s: ps(s, lo + k, lo + 1024, 8), 3, [("P", h, s, q) for q in mine], s)
        folds = [f for f in range(len(FOLD)) if FOLD[f][2] // 1024 == j]
        for f in folds:
            a, b, c0, n = FOLD[f]
            hc = helpers[f % len(helpers)]
            rid, pid, _ = topo.addr(hc)
            pi = PAIRS.index((a, b))
            qs = range(c0 // 512, (c0 + n) // 512)
            pk = [("P", h, s, q) for s in (a, b) for q in qs]
            mk = [("M", h, pi, q) for q in qs]
            lf = "lf%d%d" % (h, j)
            tr = RemoteDMATransfer(dst_ids=[DstId(rid=rid, pnc=pid)], dma_engine_mask=topo.mask(core, hc), remote_sem=sem["ha%d%d" % (f, h)],
                                   srcs=[ps(a, c0, c0 + n), ps(b, c0, c0 + n)], dsts=[helper_slot(T, v, h, f)], alu_op=2)
            op("G", 700, lambda o, tr=tr, lf=lf: g.remote_dma_fused([tr], local_sem=sem[lf]), pk, mk + [("f1", v, h, f)],
               sig=(None, 0), tag=("fold", v, h, f))
            op("D", FOLD_NS * n / 1024, None, pk + [("f1", v, h, f)], [("f2", v, h, f)],
               sig=(lf, (v + 1) * len(topo.engines(core, hc)) * len(folds)))
            op("E", 0, None, [("f2", v, h, f)], mk, lat=BACK_NS + FOLD_NS * n / 2048,
               sig=("hb%d%d" % (f, h), (v + 1) * len(topo.engines(hc, core))))
        for q in (mine if MP == 512 else mine[0:1]):
            c0, qs = 512 * q, range(q, q + MP // 512)
            for b in range(1, 4):
                todo = [a for a in range(b) if not [x for x in FOLD if x[0:2] == (a, b) and x[2] <= c0 < x[2] + x[3]]]
                if not todo:
                    continue
                crot[0] += 1
                base, bk = (512 * (crot[0] % 2), ["C%d" % (crot[0] % 2)]) if MP == 512 else (0, ["C0", "C1"])
                pe([(pC[:, base + i:base + i + 512], I1, ps(b, c0 + i, c0 + i + 512), True, True, 512) for i in range(0, MP, 512)],
                   [("P", h, b, x) for x in qs] + ["ID0"], bk, bk)
                for a in todo:
                    pi = PAIRS.index((a, b))
                    tt(M[:, 2048 * pi + c0:2048 * pi + c0 + MP], pC[:, base:base + MP], ps(a, c0, c0 + MP),
                       A.max, MP, bk + [("P", h, a, x) for x in qs], [("M", h, pi, x) for x in qs], bk)
        for pi in range(6):
            add_sums(lambda k, pi=pi: M[:, 2048 * pi + lo + k:2048 * pi + lo + 1024:8], pi // 2, [("M", h, pi, q) for q in mine], 4 + pi)
        for o in ops[first:]:
            o["long"] = o["eng"] in "SVP"

    def decide(v, h, j):
        pT, fm = T["pT%d" % j], T["fm%d" % h]
        c = slice(64 * j, 64 * j + 64)
        CT = T.CT[:, j, :]
        MS, LM, AT, cb, sg = T["MS%d" % h], T.LM, T.AT, T.cb[:, c], T.sg[:, c]
        ak, dk = [[(n, j, i) for i in range(4)] for n in "AD"]
        ms = ("MS", h, j)

        def k(name):
            return (name, j)
        cp(CT, pT[:, 0:192], 192, [("Ts", j, n) for n in range(10)] + [("Tz", j)], [k("CT")], ["T%d" % j])
        pe([(pA[64 * x:64 * x + 64, p, c], T.CT[:, j, 64 * p:64 * p + 64], ID[:, x:128:2], True, True, 64) for p in range(3) for x in range(2)],
           [k("CT"), "ID0"], ak[0:3], ["A"])
        cp(MS[:, :, c], pA[:, 0:3, c], 192, ak[0:3], [ms], ["A"])
        pe(group(pD[:, 0, c], [(wp[p], MS[:, p, c]) for p in range(3)]), ["WP", ms], dk[0:1], ["D"])
        act(sg, pD[:, 0, c], F.Sign, 64, dk[0:1], [k("sg")], ["D"], bias=0.5)
        mm = []
        for p in range(3):
            mm += group(pA[:, p, c], [(wp[3], MS[:, p, c]), (wt[1 + p], sg)])
        pe(mm, ["WP", "WT0", ms, k("sg")], ak[0:3], ["A"])
        pe(group(pD[:, 3, c], [(wt[0], sg)]), ["WT0", k("sg")], dk[3:], ["D"])
        ts(LM[:, :, c], pA[:, 0:3, c], -2048.0, 0.0, A.add, A.max, 192, ak[0:3], [k("LM")], ["A"])
        act(cb, pD[:, 3, c], F.Relu, 84, dk[3:], [k("cb"), k("acc")], ["D"], bias=-3.0, accum_out=T.acc[:, j:j + 1])
        mm = []
        for q in range(3):
            mm += group(pD[:, q, c], [(wb[3 + q], LM[:, p, c]) for p in range(3)])
        pe(mm, wbk + [k("LM")], dk[0:3], ["D"])
        act(T.ps[:, :, c], pD[:, 0:3, c], F.Sign, 192, dk[0:3], [k("ps")], ["D"], bias=0.5)
        mm = []
        for i in range(2):
            mm += group(pA[:, i, c], [(wb[7 + i], cb)] + [(wt[4 + q], T.ps[:, q, c]) for q in range(3)])
        pe(mm, wbk + ["WT1", k("ps"), k("cb")], ak[0:2], ["A"])
        act(AT[:, :, c], pA[:, 0:2, c], F.Relu, 128, ak[0:2], [k("AT")], ["A"], bias=-16.0)
        mm = group(pD[:, 0, c], [(wb[11], cb), (wb[9], AT[:, 0, c])]) + group(pD[:, 1, c], [(wb[12], cb), (wb[9], AT[:, 1, c])])
        for i in (2, 3):
            mm += group(pD[:, i, c], [(wb[13], cb), (wb[10], AT[:, 0, c])])
        pe(mm, wbk + [k("cb"), k("AT")], dk, ["D"])
        act(fm[:, :, c], pD[:, :, c], F.Copy, 256, dk, [("fm", h, j)], ["D"])

    def blend(v, h, xr):
        X, AT = T["X%d" % h], T.AT
        last = v == VI - 1
        twin = TWIN_SCATTER and not last
        n = 2 if twin else 1
        at = [("AT", 0), ("AT", 1)]
        for i in range(n):
            pe(group(pA[:, 3, 8 * i:8 * i + 8], [(I1, T.CK[:, 8 * i:8 * i + 8])] +
                     [(T.MI[:, 144 * i + 15 - r:144 * i + 143 - r], AT[:, 0, r:128:16]) for r in range(16)], 64),
               ["MI0", "MI1", "ID0", "CK0", "CK1"] + at, [("Ax", i)], ["A"])
        ts(T.ix[:, 0:8], pA[:, 3, 0:8], cx[11], None, A.add, None, 8, ["CX11", ("Ax", 0)], ["ix0"], ["A"])
        cp(T.ix[:, 8:8 + 8 * n], pA[:, 3, 0:8 * n], 16, [("Ax", 0), ("Ax", 1)], ["ix1"], ["A"])
        act(T.bg[:], X[:, 0:6144].indirect(T.ix[:, 0:16]), F.Copy, 256 * GCY, xr + [("P", h, 0, q) for q in range(4)] + ["ix0", "ix1"], ["bg"])
        mm = []
        for i in range(n):
            mm += group(pK[:, 2 + i, :], [((I1, SW)[i], T.bg[:, 0:128]), ((I1, SW)[i], T.bg[:, 128:256])], 128)
        pe(mm, ["bg", "ID0", "ID6"], ["Kb"], ["K"])
        act(T.br[:, 0:128 * n], pK[:, 2:2 + n, :], F.Identity, 128 * n, ["Kb"], ["br"], ["K"], scale=0.5, bias=127.8)
        xk = [("X", h, 0), ("X", h, 1)]
        tt(X[:, 0:4096].indirect(T.ix[:, 8:8 + 8 * n]), T.br[:, 0:128 * n], T.NEG[:, 0:128 * n], A.add, 128 * n * SCAT,
           ["br", "NEG", "ix1"], xk + (xr if v == 0 else []))
        for t in range(2):
            mine = X[64 * t:64 * t + 64, 2048 * t:2048 * t + 2048]
            if last:
                dma("Y", T.yx[64 * h:64 * h + 64, 2048 * t:2048 * t + 2048], mine, "out", OUTS, [("X", h, t)], (), 3000)
            elif not twin:
                dma("Y", X[64 - 64 * t:128 - 64 * t, 2048 * t:2048 * t + 2048], mine, "tw%d" % h, 32 * (v + 1), (), [("X", h, t)], 3500)
        if not last:
            a = pA[:, 3, 64:65]
            pe(group(a, [(T.AW[:], T.acc[:, 0:1]), (T.AW[:], T.acc[:, 1:2])], 256), ["AW", ("acc", 0), ("acc", 1)], ["Aa"], ["A"])
            cp(T.ai[:, h:h + 1], a, 1, ["Aa"], [("ai", h)], ["A"])
            ts(T.ai[:, h:h + 1], T.ai[:, h:h + 1], 31, None, A.bitwise_and, None, 1, (), [("ai", h)])

    def strands(v, h, j):
        MS, fm, U = T["MS%d" % h], T["fm%d" % h], T["U%d" % h]
        SC, R = T["SC%d" % h], T["R%d" % h]
        c = slice(64 * j, 64 * j + 64)
        last = v == VI - 1
        s = [SC[:, v, i, c] for i in range(7)]
        sk = [("SC", v, h, j, i) for i in range(7)]
        nx = [SC[:, v + 1, i, c] for i in range(7)]
        nk = [("SC", v + 1, h, j, i) for i in range(7)]
        ek, kk = [[(n, j, i) for i in range(4)] for n in "EK"]
        thr, f, ov, HC, ms = T["thr%d" % h][:, 0:1], ("fm", h, j), T.ov[:, c], T.HC, ("MS", h, j)
        idk = ["ID0", "ID1"]
        f02, e01, e23, k01 = fm[:, 0:2, c], pE[:, 0:2, c], pE[:, 2:4, c], pK[:, 0:2, c]

        def k(name):
            return (name, j)
        pe(group(pE[:, 0, c], [(I1, s[2]), (NI, s[1])]) + group(pE[:, 1, c], [(I1, s[2]), (NI, s[3])]) +
           group(pE[:, 2, c], [(PM, MS[:, 0, c]), (NPM, MS[:, 1, c])]) + group(pE[:, 3, c], [(PM, MS[:, 2, c]), (NPM, MS[:, 1, c])]),
           idk + sk[1:4] + [ms, "PM", "NPM"], ek, ["E"])
        tt(T.FM[:, :, c], f02, e23, A.mult, 128, [f] + ek[2:], [k("FM")], ["E"])
        pe(group(pE[:, 2, c], [(PM, MS[:, 1, c]), (I1, T.FM[:, 0, c]), (I1, T.FM[:, 1, c])]), [ms, "PM", "ID0", k("FM")], ek[2:3], ["E"])
        tt(k01, f02, e01, A.mult, 128, [f] + ek[0:2], kk[0:2], ["E", "K"])
        tt(SC[:, v, 4:6, c], SC[:, v, 1:4:2, c], k01, A.add, 128, kk[0:2] + [sk[1], sk[3]], sk[4:6], ["K"])
        ts(ov, pE[:, 2, c], thr, None, A.is_gt, None, 64, ek[2:3] + [("thr", h)], [k("ov")], ["E"])
        if not last and j == 1:
            tt(thr, T.ai[:, h:h + 1], T["thi%d" % h][:, 0:1], A.add, 1, [("ai", h)], [("thr", h)])
        one = T.ONE[:, 0:64]
        pe(group(pE[:, 0, c], [(I1, s[0]), (I4096, ov)]) + group(pE[:, 1, c], [(I1, s[4]), (I4096, ov)]) +
           group(pE[:, 2, c], [(I2048, one), (I1, s[1]), (I1, s[2]), (I1, s[3]), (NI, s[4]), (NI, s[5])]) +
           group(pE[:, 3, c], [(I2048, one), (I1, s[5])]), idk + ["ID3", "ID4", "ONE", k("ov")] + sk[0:6], ek, ["E"])
        act(T.mm[:, :, c], e01, F.Relu, 128, ek[0:2], [k("mm")], ["E"], bias=-2048.0)
        pe(group(pK[:, 0, c], [(IOFF, one), (I32, s[1]), (I32, s[2]), (I32, s[3]), (N32, s[4]), (N32, s[5]), (W37, ov)]) +
           group(pK[:, 1, c], [(IOFF, one), (I32, s[5]), (W37, ov)]), ["ID2", "ID5", "ID7", "W37", "ONE", k("ov")] + sk[1:6], kk[0:2], ["K"])
        PR, TI = T.PR[:, :, c], T.TI[:, :, c]
        tt(PR, T.mm[:, :, c], e23, A.mult, 128, [k("mm")] + ek[2:], [k("PR")], ["E"])
        tt(TI, PR, k01, A.add, 128, [k("PR")] + kk[0:2], [k("TI")], ["K"])
        ts(TI, TI, 5, 4095, A.arith_shift_right, A.bitwise_and, 128, (), [k("TI")])
        ts(HC[:, :, c], TI, -2048.0, None, A.add, None, 128, [k("TI")], [k("HC")])
        pe(group(pE[:, 0, c], [(NI, s[0]), (I1, HC[:, 0, c])]) + group(pE[:, 1, c], [(NI, s[4]), (I1, HC[:, 1, c])]),
           idk + [k("HC"), sk[0], sk[4]], ek[0:2], ["E"])
        tt(k01, fm[:, 2:4, c], e01, A.mult, 128, [f] + ek[0:2], kk[0:2], ["E", "K"])
        tt(SC[:, v + 1, 0:5:4, c], SC[:, v, 0:5:4, c], k01, A.add, 128, kk[0:2] + [sk[0], sk[4]], [nk[0], nk[4]], ["K"])
        tt(SC[:, v + 1, 5:7, c], HC[:, :, c], k01, A.subtract, 128, kk[0:2] + [k("HC")], nk[5:7], ["K"])
        pe(group(pE[:, 2, c], [(NI, nx[4]), (I1, nx[5])]) + group(pE[:, 3, c], [(I1, nx[5]), (NI, nx[6])]), idk + nk[4:7], ek[2:], ["E"])
        tt(k01, f02, e23, A.mult, 128, [f] + ek[2:], kk[0:2], ["E", "K"])
        rk = [("R", v, h, j, i) for i in range(4)]
        tt(R[:, v, 1:4:2, c], SC[:, v + 1, 4:7:2, c], k01, A.add, 128, kk[0:2] + [nk[4], nk[6]], [rk[1], rk[3]], ["K"])
        tt(T.o2[:, 0, c], nx[5], pK[:, 0, c], A.subtract, 64, kk[0:1] + [nk[5]], [k("o2")], ["K"])
        tt(R[:, v, 2, c], T.o2[:, 0, c], pK[:, 1, c], A.subtract, 64, kk[1:2] + [k("o2")], [rk[2]], ["K"])
        if not last:
            ts(U[:, 0, c], nx[0], 2048.0, None, A.add, None, 32, [nk[0]], [("U", h, j, 0)])
        if JOIN and j == 0:
            return
        js = (0, 1) if JOIN else (j,)
        c = slice(64 * js[0], 64 * js[-1] + 64)
        arr = ["ar%d%d%d%d" % (v, h, j, i) for i in range(4)]
        trs = []
        for i in (1, 2, 3):
            rid, pid, _ = topo.addr(others[i])
            trs.append(RemoteDMATransfer(dst_ids=[DstId(rid=rid, pnc=pid)], dma_engine_mask=bits(masks[i]), remote_sem=sem[arr[i]],
                                         src=R[:, v, i, c], dst=SC[:, v + 1, i, c]))
        op("G", 900, lambda o: g.remote_dma_fused(trs, local_sem=sem.sent), [("R", v, h, q, i) for q in js for i in (1, 2, 3)],
           [("mv", v, h, j)], sig=(None, 0))
        op("D", SEND_BUSY, None, [("mv", v, h, j)], [("mw", v, h, j)], sig=("sent", sent * (2 if JOIN else 4) * VI))
        for i in (1, 2, 3):
            op("E", 0, None, [("mw", v, h, j)], [("SC", v + 1, h, q, i) for q in js], lat=SEND_NS - 1000 * (i in near), sig=(arr[i], len(masks[i])))
        n = 64 * len(js)
        if not last:
            ts(U[:, 1:4, c], SC[:, v + 1, 1:4, c], 2048.0, None, A.add, None, 1.5 * n,
               [("SC", v + 1, h, q, i) for q in js for i in (1, 2, 3)], [("U", h, q, i) for q in js for i in (1, 2, 3)])
            return
        OF = T["OF%d" % h]
        for i in (0, 2, 1, 3):
            ts(OF[:, i, c], SC[:, v + 1, i, c], 2048.0, None, A.add, None, n, [("SC", v + 1, h, q, i) for q in js], [("OF", h, j, i)])
            for t in range(2):
                c0 = 256 * i + 128 * t + 64 * js[0]
                dma("S" if (h and t) else "Y", T.ys[64 * h:64 * h + 64, c0:c0 + n], OF[64 * t:64 * t + 64, i, c],
                    "out", OUTS, [("OF", h, j, i)], (), 2200)

    for v in range(VI):
        for h in range(2):
            cur[0] = 2 * v + h
            xr = [("X" if v else "Xl", h, t) for t in range(2)]
            if v == 0:
                for s in (0, 2, 1, 3):
                    hk = [("HI", h, s, t) for t in range(2)]
                    cp(T["U%d" % h][:, s, :], T["HI%d" % h][:, s, :], 128, hk, [("U", h, j, s) for j in range(2)])
                hk = [("HI", h, s, t) for t in range(2) for s in range(4)]
                ts(T["SC%d" % h][:, 0, 0:4, :], T["HI%d" % h][:], -2048.0, None, A.add, None, 512, hk,
                   [("SC", 0, h, j, s) for j in range(2) for s in range(4)])
            for j in range(2):
                costs(v, h, j, xr)
            for j in range(2):
                decide(v, h, j)
            blend(v, h, xr)
            for j in range(2):
                strands(v, h, j)
    return ops


def schedule(ops):
    if "order" not in PLAN:
        pred = [sorted(o["deps"]) for o in ops]
        succ = [[] for _ in ops]
        for i, p in enumerate(pred):
            for d in p:
                succ[d].append(i)
        tail = [0.0] * len(ops)
        for o in reversed(ops):
            tail[o["i"]] = o["dur"] + o["lat"] + 120 + max([tail[s] for s in succ[o["i"]]] + [0.0])
        for look, lead, bonus in TRIES:
            prio = [tail[o["i"]] + lead * (o["h"] == 0) - bonus * o["long"] for o in ops]
            for n in range(ROUNDS):
                order, start, fin = place(ops, pred, succ, prio, look, False)
                if max(fin) < PLAN.get("end", 1e18):
                    PLAN.update({"order": order, "end": max(fin), "start": start, "by": (look, lead, bonus, n)})
                if n + 1 < ROUNDS:
                    prio = place(ops, succ, pred, fin, look, True)[2]
                    prio = [p - bonus * o["long"] for p, o in zip(prio, ops)]
    bank, lastacc = {}, {}
    for i in PLAN["order"]:
        o = ops[i]
        o["t"] = PLAN["start"][i]
        if o["tag"] is not None and o["tag"][0] == "acc":
            lastacc[o["tag"]] = i
        for b in o["banks"]:
            for e2, d in bank.get(b, {}).items():
                if e2 != o["eng"]:
                    o["deps"].add(d)
            bank.setdefault(b, {})[o["eng"]] = i
    for i in lastacc.values():
        ops[i]["stop"] = True
    return PLAN["order"], PLAN["end"]


PLAN = {}


def place(ops, pred, succ, prio, look, back):
    n = len(ops)
    left = [len(p) for p in pred]
    base, fin, start = [0.0] * n, [0.0] * n, [0.0] * n
    free, bank, order, avail = {}, {}, [], {}
    for i in range(n):
        if not left[i]:
            avail.setdefault(ops[i]["eng"], []).append(i)
    while len(order) < n:
        best = None
        for e, l in avail.items():
            if not l:
                continue
            c = []
            for i in l:
                t = max(base[i], free.get(e, 0.0))
                for b in ops[i]["banks"]:
                    for e2, d in bank.get(b, {}).items():
                        if e2 != e:
                            t = max(t, fin[d] + CROSS)
                c.append((t, i))
            t0 = min(c)[0]
            if best is None or t0 < best[0]:
                best = (t0, e, c)
        t0, e, c = best
        t, i = max([x for x in c if x[0] <= t0 + look], key=lambda x: prio[x[1]])
        o = ops[i]
        start[i] = t
        for b in o["banks"]:
            bank.setdefault(b, {})[e] = i
        if e != "E":
            free[e] = t + o["dur"]
        fin[i] = t + o["dur"] + (0 if back else o["lat"])
        order.append(i)
        avail[e].remove(i)
        for s in succ[i]:
            e2 = ops[s]["eng"]
            gap = 0 if (e if back else e2) in "DE" else SAME if e2 == e else CROSS
            base[s] = max(base[s], fin[i] + gap + (ops[s]["lat"] if back else 0))
            left[s] -= 1
            if left[s] == 0:
                avail.setdefault(e2, []).append(s)
    return order, start, fin


def rank_program(g, core, T, topo):
    rank = T.rank_of(core)
    if rank is None:
        owner = [c for c in T.cores if core in helpers_of(c, T, topo)]
        if not owner or not FOLD:
            return
        owner = owner[0]
        hs = helpers_of(owner, T, topo)
        ops = build(g, owner, T, topo)
        order, _ = schedule(ops)
        rid, pid, _ = topo.addr(owner)
        ne, total = len(topo.engines(core, owner)), 0
        for i in order:
            tag = ops[i]["tag"]
            if tag is None or tag[0] != "fold" or hs[tag[3] % len(hs)] != core:
                continue
            v, h, f = tag[1:]
            c0 = 2048 * PAIRS.index(FOLD[f][0:2]) + FOLD[f][2]
            g.wait_ge(T.sem["ha%d%d" % (f, h)], (v + 1) * len(topo.engines(owner, core)))
            g.remote_dma(T["M%d" % h][:, c0:c0 + FOLD[f][3]], helper_slot(T, v, h, f), T.sem["hb%d%d" % (f, h)],
                         T.sem.hsent, pid, rid, topo.mask(core, owner))
            total += ne
        if total:
            g.wait_ge(T.sem.hsent, total)
        return
    ops = build(g, core, T, topo)
    order, _ = schedule(ops)
    queue = {"V": g.vector, "S": g.scalar, "P": g.tensor, "G": g, "Y": g.sync}
    needed = set()
    for o in ops:
        for d in o["deps"]:
            if o["fn"] is not None and not (o["eng"] == "P" and ops[d]["eng"] == "P"):
                needed.add(d)
    count, waited, totals = {}, {}, {}
    for i in order:
        o = ops[i]
        e = o["eng"]
        mark = False
        if o["sig"] is None:
            if i in needed:
                count[e] = count.get(e, 0) + 1
                mark = True
            o["sig"] = ("c" + e, count.get(e, 0))
        if o["sig"][0] is not None:
            totals[o["sig"][0]] = max(totals.get(o["sig"][0], 0), o["sig"][1])
        if o["fn"] is None:
            continue
        want = {}
        for d in o["deps"]:
            s, val = ops[d]["sig"]
            if s is None or (e == "P" and ops[d]["eng"] == "P"):
                continue
            want[s] = max(want.get(s, 0), val)
        for s in sorted(want):
            if want[s] > waited.get((e, s), 0):
                queue[e].wait_ge(T.sem[s], want[s])
                waited[(e, s)] = want[s]
        ins = o["fn"](o)
        if mark:
            ins.then_inc(T.sem["c" + e], 1)
    for s in sorted(totals):
        if totals[s] > waited.get(("G", s), 0):
            g.wait_ge(T.sem[s], totals[s])
